import numpy as np, ml_dtypes
CORES = [1,5,17,21,33,37,49,53]
N = 8
import mx_ref
BF = ml_dtypes.bfloat16
def entries(a):
    return np.ascontiguousarray(a.T).reshape(-1)
def table(e):
    return np.ascontiguousarray(np.reshape(e, (-1, 16)).T).astype(np.int32)
def cols(t, e):
    v = np.concatenate([t.reshape(128, -1, 4), np.zeros((128, 1, 4), BF)], axis=1)
    return np.ascontiguousarray(v[:, e]).reshape(128, -1)
def cut(t, i, w=512):
    return t[:, w * i:w * i + w]
def f(rng, *shape):
    return mx_ref.flush((rng.standard_normal(shape, dtype=np.float32) * np.exp2(rng.integers(-2, 3, shape[:-1] + (1,)))).astype(BF))
def wide(rng, *shape, cols=0):
    v = rng.standard_normal(shape, dtype=np.float32) * np.exp2(rng.integers(-12, 13, shape)).astype(np.float32)
    if cols: v *= np.repeat(np.exp2(rng.integers(-cols, cols + 1, shape[:-2] + (1, shape[-1] // 4))) * (rng.random(shape[:-2] + (1, shape[-1] // 4)) > 0.0625), 4, axis=-1).astype(np.float32)
    return mx_ref.flush(v.astype(BF))
T, O = 384, 1
def places(rng, dest):
    e = np.zeros((N, T), int)
    for d in range(N): e[dest == d] = d * T + rng.permutation(T)
    return np.stack([table(e[r]) for r in range(N)])
def relabel(rng):
    p = rng.permutation(N)
    if np.all((p - np.arange(N)) % N == p[0]): p[[0, 1]] = p[[1, 0]]
    return p
def setup_inputs(rng):
    e = rng.permutation(N * T).reshape(N, T)
    return {"x": f(rng, N, 128, 4 * T), "to": np.stack([table(e[r]) for r in range(N)]), "w": f(rng, N, 128, 512 * O)}
def setup_inputs_swap(rng):
    d = setup_inputs(rng); p = rng.permutation(N); dest = np.zeros((N, T), int)
    for k in range(N): dest[p[k]] = p[(k + 1) % N]
    d["to"] = places(rng, dest); return d
def setup_inputs_ones(rng):
    d = setup_inputs(rng); i = np.arange(N); n = np.ones((N, N), int); n[i, rng.permutation(N)] += T % N
    for t in range(T // N - 1): n[i, rng.permutation(N)] += N
    d["to"] = places(rng, np.stack([rng.permutation(np.repeat(i, n[r])) for r in range(N)])); return d
def setup_inputs_runs(rng):
    d = setup_inputs(rng); p = relabel(rng); s, u = rng.integers(1, N), rng.integers(0, N); g, h = rng.permutation(N), rng.permutation(N)
    n = T // N + ((g[:, None] + h) % N < T % N)
    j = (np.arange(N) + s * np.arange(N)[:, None] + u) % N
    d["to"] = places(rng, np.stack([np.repeat(p[j[r]], n[r, j[r]]) for r in range(N)])); return d
def setup_inputs_comb(rng):
    d = setup_inputs(rng); p = relabel(rng); s, u = rng.integers(1, N), rng.integers(0, N); k = rng.permutation(N); c = np.arange(T)
    d["to"] = places(rng, np.stack([p[(c + np.where(c < T - T % N, s * r + u, k[r])) % N] for r in range(N)])); return d
def setup_inputs_spread(rng):
    d = setup_inputs(rng); d["x"] = wide(rng, N, 128, 4 * T, cols=8); return d
def check_inputs(d):
    e = np.concatenate([entries(d["to"][r]) for r in range(N)])
    return [] if np.array_equal(np.sort(e), np.arange(N * T)) else ["to"]
def reference(x, to, w):
    z = np.concatenate([x[r] for r in range(N)], axis=1)
    e = np.concatenate([entries(to[r]) for r in range(N)])
    home = np.zeros(N * T, int); home[e] = np.arange(N * T)
    y = np.zeros((N, 128, O * T), np.float32)
    for d in range(N):
        v = mx_ref.quantize(cols(z, home[d * T:d * T + T]))
        for o in range(O): y[d][:, T * o:T * o + T] = mx_ref.matmul(mx_ref.quantize(np.ascontiguousarray(cut(w[d], o))), v)
    return {"y": y}

@@ -1,0 +1,439 @@
+from concourse.bass import DstId, RemoteDMATransfer
+from concourse.mybir import dt, AluOpType as A, ActivationFunctionType as AF
+
+T0, N, Q1, CAP, SW = 384, 8, 48, 56, 64
+R1 = Q1 + 1
+OWN = 64
+L2 = OWN + 7 * CAP
+L1 = L2 - 2 * CAP
+NOPL = 8191.0
+BIG = 65536.0
+X4, U8, U16, F32, BF, I32 = "float8_e4m3fn_x4", "uint8", "uint16", "float32", "bfloat16", "int32"
+
+
+def sb(n, t):
+    return ("sbuf", [128, n], t)
+
+
+SCRATCH = {
+    "xt": sb(1536, BF), "wt": sb(512, BF), "qx": sb(T0, X4), "sx": sb(T0, U8), "qw": sb(128, X4), "sw": sb(128, U8),
+    "slot1c": sb(400, X4), "slot1s": sb(400, U8), "land1c": sb(512, X4), "land1s": sb(512, U8),
+    "slot2c": sb(512, X4), "slot2s": sb(512, U8), "land2c": sb(L2, X4), "land2s": sb(L2, U8),
+    "relst": sb(8, U16), "rel1c": sb(R1, X4), "rel1s": sb(R1, U8), "rel2c": sb(CAP, X4), "rel2s": sb(CAP, U8),
+    "tab": sb(24, I32), "key": sb(24, I32), "tabk": sb(32, F32), "M": sb(192, F32),
+    "W": sb(816, F32), "z192": sb(192, F32), "rst32": sb(32, F32), "rst8": sb(64, F32),
+    "gd": sb(192, F32), "td": sb(192, F32), "pos": sb(192, F32), "trr": sb(32, F32),
+    "torc": sb(T0, F32), "padr": sb(128, F32), "tt0": sb(32, F32),
+    "Qs": sb(32, F32), "tb": sb(96, F32), "tb2": sb(96, F32), "F": sb(8, F32), "off1": sb(24, U16),
+    "win1": sb(512, F32), "tr1": sb(512, F32), "Ge": sb(32, F32), "Go": sb(32, F32), "G": sb(24, F32),
+    "g1": sb(26, U16), "ownl": sb(4, U16), "srow": sb(4096, F32), "zz": sb(768, BF),
+    "pidx": sb(4, I32), "pi15": sb(4, I32), "pi16": sb(4, I32), "par15": sb(1, F32), "par128": sb(1, F32),
+    "par16": sb(1, F32), "par1": sb(1, F32), "epar": sb(1, F32), "k16": sb(4, F32), "fl4": sb(4, F32), "kp": sb(4, F32),
+    "kt": sb(4, F32), "kpo": sb(4, F32), "kpo8": sb(4, F32), "nk": sb(4, F32), "nko8": sb(4, F32), "cA": sb(64, F32),
+    "cA2": sb(64, F32), "st": sb(64, U16), "stf": sb(72, F32), "nn": sb(64, I32), "ai": sb(64, I32), "ci": sb(64, I32),
+    "ti": sb(64, I32), "c8p": sb(66, F32), "nB": sb(64, F32), "ge": sb(256, F32), "tq": sb(64, F32), "sc": sb(256, F32),
+    "off2": sb(32, U16), "nBx": sb(64, F32), "stx": sb(64, F32), "ai2": sb(64, I32), "ti2": sb(64, I32),
+    "tq2": sb(64, F32), "ge2": sb(256, F32), "sc2": sb(256, F32), "off3": sb(32, U16),
+    "sg2": sb(512, F32), "tr3": sb(512, F32), "d0": sb(64, F32), "d1": sb(64, F32), "pl": sb(64, F32), "off4": sb(32, U16),
+    "val": sb(512, BF), "valo": sb(512, BF), "win2": sb(3712, BF), "tr2": sb(416, BF), "Ie": sb(26, F32),
+    "Io": sb(26, F32), "G2": sb(24, F32), "off5": sb(24, U16), "ysb": sb(L2, F32), "yo": sb(T0, F32),
+    "sland": ("dram", [8, 128, 4], F32), "ps": ("psum", [128, 1024], F32),
+}
+SEMAPHORES = ["vq", "gc1", "gct", "gc2", "lt", "lx", "lw", "keyq", "ms", "gds", "fs", "tds", "trs", "torw", "sto", "qxs",
+              "g1s", "pk1c", "pk1s", "scq", "owns", "own1c", "own1s", "stst", "srz", "wz", "off2s", "pk2c", "pk2s",
+              "own2c", "own2s", "srl", "mm0", "mm1", "cpv", "cps", "off5s", "yv", "ys", "yst", "qws", "sst", "sls", "p1",
+              "p2a", "p2b", "loc", "zzs", "bq", "stq", "dupq", "valq", "valo", "vald", "w2s", "rst_", "r1c", "r1s", "r2c",
+              "r2s"]
+
+
+def bits(m):
+    return bin(m).count("1")
+
+
+def mask_of(es):
+    return sum(1 << x for x in es)
+
+
+def plan(topo, ranks, r):
+    me = ranks[r]
+    order = [(r + i) % N for i in range(1, N)]
+    far = [d for d in order if topo.chip(ranks[d]) != topo.chip(me)]
+    near = [d for d in order if topo.chip(ranks[d]) == topo.chip(me)]
+    hands = [c for c in topo.cores_of(me) if c not in ranks and topo.die(c) == topo.die(me)]
+    e = topo.engines(me, ranks[far[0]])
+    rest = [x for x in topo.engines(me, hands[0]) if x not in e]
+    direct = [(d, mask_of(e[2 * i:2 * i + 2])) for i, d in enumerate(far[:4])]
+    half = len(rest) // 2
+    via = [(d, hands[i], mask_of(rest[half * i:half * i + half]), topo.mask(hands[i], ranks[d]))
+           for i, d in enumerate(far[4:])]
+    return {"direct": direct, "via": via, "near": [(d, mask_of(rest)) for d in near]}
+
+
+def dst_of(topo, c):
+    a = topo.addr(c)
+    return DstId(rid=a[0], pnc=a[1])
+
+
+def base(plans, s, d):
+    cyc = [(d + k) % N for k in range(1, N)]
+    late = [q for q in cyc if d in [v[0] for v in plans[q]["via"]]]
+    order = [q for q in cyc if q not in late] + late
+    return 0 if s == d else OWN + CAP * order.index(s)
+
+
+def hand_on(g, core, T, topo, ranks, plans):
+    for s in range(N):
+        for d, c, m_in, m_out in plans[s]["via"]:
+            if c != core:
+                continue
+            b = base(plans, s, d)
+            steps = [("rst_", T.relst[:], T.st[:, 8 * s:8 * s + 8], "sst"),
+                     ("r1c", T.rel1c[:].bitcast(dt.uint8), T.land1c[:, SW * s:SW * s + R1].bitcast(dt.uint8), "p1"),
+                     ("r1s", T.rel1s[:], T.land1s[:, SW * s:SW * s + R1], "p1"),
+                     ("r2c", T.rel2c[:].bitcast(dt.uint8), T.land2c[:, b:b + CAP].bitcast(dt.uint8), "p2b"),
+                     ("r2s", T.rel2s[:], T.land2s[:, b:b + CAP], "p2b")]
+            for sem, src, dst, rsem in steps:
+                g.wait_ge(T.sem[sem], bits(m_in))
+                g.remote_dma_fused([RemoteDMATransfer(dst_ids=[dst_of(topo, ranks[d])], dma_engine_mask=m_out,
+                                                      remote_sem=T.sem[rsem], src=src, dst=dst)], local_sem=T.sem.loc)
+            g.wait_ge(T.sem.loc, len(steps) * bits(m_out))
+
+
+def rank_program(g, core, T, topo):
+    me = T.rank_of(core)
+    ranks = list(T.cores)
+    plans = [plan(topo, ranks, r) for r in range(N)]
+    if me is None:
+        hand_on(g, core, T, topo, ranks, plans)
+        return
+    V, S, Y, TE, sem = g.vector, g.scalar, g.sync, g.tensor, T.sem
+    vn, ln = [0], [0]
+    mine = plans[me]
+
+    def v(ins, name=None):
+        if name is None:
+            ins.then_inc(sem.vq, 1)
+            vn[0] += 1
+        else:
+            ins.then_inc(sem[name], 1)
+
+    def vw():
+        V.wait_ge(sem.vq, vn[0])
+
+    def ts(out, in0, s1, s2, o0, o1=None, name=None):
+        v(V.tensor_scalar(out, in0, s1, s2, o0, o1) if o1 is not None else V.tensor_scalar(out, in0, s1, s2, o0), name)
+
+    def tt(out, a, b, op, name=None):
+        v(V.tensor_tensor(out, a, b, op), name)
+
+    def cp(out, in_, name=None):
+        v(V.tensor_copy(out, in_), name)
+
+    def scan(out, a, b, o0, o1, name=None):
+        v(V.tensor_tensor_scan(out, a, b, 0.0, o0, o1), name)
+
+    def fused(trs):
+        g.remote_dma_fused([RemoteDMATransfer(dst_ids=[dst_of(topo, c) for c in cs], dma_engine_mask=m, remote_sem=sem[rs],
+                                              srcs=[s], dsts=[d for c in cs]) for cs, m, rs, s, d in trs], local_sem=sem.loc)
+        ln[0] += sum(bits(t[1]) for t in trs)
+
+    def send_far(src, dst, rel, rsem, relsem):
+        fused([([ranks[d]], m, rsem, src(d), dst(d)) for d, m in mine["direct"]]
+              + [([c], m, relsem, src(d), rel) for d, c, m, mo in mine["via"]])
+
+    def send_near(src, dst, rsem):
+        fused([([ranks[d]], m, rsem, src(d), dst(d)) for d, m in mine["near"]])
+
+    def incoming(kinds):
+        return sum(bits(t[-1]) for r in range(N) for k in kinds for t in plans[r][k] if t[0] == me)
+    every = ("direct", "near", "via")
+
+    all_mask = topo.mask(core, ranks[mine["direct"][0][0]])
+    nsl = bits(all_mask) * (N - 1)
+
+    for q in range(8):
+        (Y if q % 2 == 0 else S).dma_start(T.tab[16 * q:16 * q + 16, :], T.to[:]).then_inc(sem.lt, 16)
+    S.dma_start(T.xt[:], T.x[:]).then_inc(sem.lx, 16)
+
+    def iota(out, pat, b, cm, s):
+        g.iota(out, pat, b, cm, allow_small_or_imprecise_dtypes=True).then_inc(sem[s], 1)
+    g.iota(T.pidx[:], [[0, 4]], 0, 1).then_inc(sem.gc1, 1)
+    iota(T.torc[:], [[1, T0]], 0, 0, "gct")
+    iota(T.k16[:], [[16, 4]], 0, 0, "gc2")
+    iota(T.fl4[:], [[0, 2], [-32, 2]], 16, 0, "gc2")
+    iota(T.cA[:], [[0, 8], [512, 8]], 7 - me, 0, "gc2")
+    iota(T.cA2[:], [[-1, 8], [512, 8]], 7, 0, "gc2")
+    iota(T.d1[:, 1:64:2], [[16, 32]], N * T0, 1, "gc2")
+
+    v(V.memset(T.zz[:], 0.0), "zzs")
+    v(V.memset(T.padr[:], NOPL), "wz")
+    v(V.memset(T.W[:, 23:791:24], 0.0))
+    v(V.memset(T.tabk[:], 0.0))
+    v(V.memset(T.z192[:], 0.0))
+    v(V.memset(T.rst32[:], 1.0))
+    v(V.memset(T.g1[:], 0))
+    v(V.memset(T.ownl[:], 0))
+    V.wait_ge(sem.gc1, 1)
+    ts(T.pi15[:], T.pidx[:], 15, None, A.bitwise_and)
+    ts(T.pi16[:], T.pidx[:], 16, None, A.bitwise_and)
+    vw()
+    v(V.memset(T.rst32[:, 0:32:16], 0.0))
+    ts(T.par128[:], T.pi16[:, 0:1], 8.0, -1.0, A.mult, A.add)
+    ts(T.par1[:], T.pi16[:, 0:1], 0.0625, None, A.mult)
+    ts(T.epar[:], T.pi16[:, 0:1], -0.0625, 1.0, A.mult, A.add)
+    v(V.memset(T.win1[:], 0.0))
+    S.wait_ge(sem.zzs, 1)
+    for h in range(2):
+        S.activation(T.srow[:, 768 * h:768 * h + 768], T.zz[:], AF.Copy).then_inc(sem.srz, 1)
+
+    vw()
+    V.wait_ge(sem.lt, 128)
+    cp(T.tabk[:, 0:24], T.tab[:], "gds")
+    ts(T.key[:], T.tab[:], 1.0 / T0, 0.5 / T0 - 0.5, A.mult, A.add, name="keyq")
+    V.wait_ge(sem.gds, 1)
+    v(V.transpose(T.trr[:], T.tabk[:]), "trs")
+    V.wait_ge(sem.keyq, 1)
+    for d in range(N):
+        ts(T.M[:, 24 * d:24 * d + 24], T.key[:], float(d), None, A.is_equal, name="ms")
+    Y.wait_ge(sem.trs, 1)
+    Y.wait_ge(sem.gct, 1)
+    Y.dma_start(T.torc[1:2, :], T.trr[0:24, 0:16]).then_inc(sem.torw, 16)
+    Y.dma_start(T.wt[:], T.w[:]).then_inc(sem.lw, 16)
+    V.wait_ge(sem.ms, N)
+    scan(T.W[:, 24:216], T.M[:], T.z192[:], A.add, A.add)
+    S.wait_ge(sem.gds, 1)
+    for d in range(N):
+        S.activation(T.gd[:, d:192:8], T.tabk[:, 0:24], AF.Identity, 512.0 - 1024.0 * T0 * d, 1024.0).then_inc(sem.gds, 1)
+    vw()
+    v(V.transpose(T.tt0[:], T.W[:, 23:791:24]))
+    vw()
+    scan(T.Qs[:], T.rst32[:], T.tt0[:], A.mult, A.add)
+    vw()
+    ts(T.tb[:, 0:32], T.Qs[:], -1.0, T.Qs[:, 15:16], A.mult, A.add)
+    tt(T.tb[:, 32:64], T.Qs[:], T.tt0[:], A.subtract)
+    vw()
+    v(V.transpose(T.tb2[:, 0:64], T.tb[:, 0:64]))
+    ts(T.tb[:, 64:96], T.Qs[:], 0.0, T.Qs[:, 15:16], A.mult, A.add)
+    vw()
+    tt(T.F[:], T.tb2[:, 0:8], T.tb2[:, 33:41], A.add, "fs")
+    v(V.transpose(T.tb2[:, 64:96], T.tb[:, 64:96]))
+    V.wait_ge(sem.fs, 1)
+    S.wait_ge(sem.fs, 1)
+    for d in range(5):
+        ts(T.td[:, d:192:8], T.W[:, 24 + 24 * d:48 + 24 * d], T.F[:, d:d + 1], None, A.add)
+    for d in range(5, N):
+        S.activation(T.td[:, d:192:8], T.W[:, 24 + 24 * d:48 + 24 * d], AF.Identity, T.F[:, d:d + 1]).then_inc(sem.tds, 1)
+    vw()
+    cp(T.st[:, 8 * me:8 * me + 8], T.tb2[:, 64:72], "sto")
+    V.wait_ge(sem.tds, N - 5)
+    V.wait_ge(sem.gds, N + 1)
+    scan(T.pos[:], T.gd[:], T.td[:], A.max, A.min)
+    vw()
+    ts(T.off1[:], T.pos[:, 7:192:8], T.par128[:], None, A.add)
+    V.wait_ge(sem.gct, 1)
+    V.wait_ge(sem.torw, 16)
+    vw()
+    cp(T.win1[:].indirect(T.off1[:, 0:24]), T.torc[:], "scq")
+    V.wait_ge(sem.lx, 16)
+    v(V.quantize_mx(T.qx[:], T.sx[:], T.xt[:]), "qxs")
+    V.wait_ge(sem.scq, 1)
+    for m in range(N):
+        v(V.transpose(T.tr1[:, 64 * m:64 * m + 64], T.win1[:, m:512:8]))
+    vw()
+    ts(T.Ge[:], T.tr1[:, 0:512:16], T.epar[:], None, A.mult)
+    ts(T.Go[:], T.tr1[:, 0:512:16], T.par1[:], None, A.mult)
+    vw()
+    tt(T.G[:, 0:24:3], T.Ge[:, 0:32:4], T.Go[:, 1:32:4], A.add)
+    tt(T.G[:, 1:24:3], T.Ge[:, 3:32:4], T.Go[:, 0:32:4], A.add)
+    tt(T.G[:, 2:24:3], T.Ge[:, 2:32:4], T.Go[:, 3:32:4], A.add)
+    vw()
+    cp(T.g1[:, 0:24], T.G[:], "g1s")
+    cp(T.ownl[:, 0:3], T.G[:, 3 * me:3 * me + 3], "owns")
+    V.wait_ge(sem.g1s, 1)
+    V.wait_ge(sem.qxs, 1)
+    cp(T.slot1c[:].bitcast(dt.uint32), T.qx[:].bitcast(dt.uint32).indirect(T.g1[:, 0:25]), "pk1c")
+    for h in range(2, 4):
+        S.activation(T.srow[:, 768 * h:768 * h + 768], T.zz[:], AF.Copy).then_inc(sem.srz, 1)
+    S.wait_ge(sem.g1s, 1)
+    S.wait_ge(sem.qxs, 1)
+    S.activation(T.slot1s[:], T.sx[:].indirect(T.g1[:, 0:25]), AF.Copy).then_inc(sem.pk1s, 1)
+    V.wait_ge(sem.owns, 1)
+    own1 = slice(SW * me, SW * me + SW)
+    cp(T.land1c[:, own1].bitcast(dt.uint32), T.qx[:].bitcast(dt.uint32).indirect(T.ownl[:]), "own1c")
+    S.wait_ge(sem.owns, 1)
+    S.activation(T.land1s[:, own1], T.sx[:].indirect(T.ownl[:]), AF.Copy).then_inc(sem.own1s, 1)
+    for lo, hi in ((3072, 3840), (3840, 4096)):
+        S.activation(T.srow[:, lo:hi], T.zz[:, 0:hi - lo], AF.Copy).then_inc(sem.srz, 1)
+    Y.wait_ge(sem.wz, 1)
+    Y.dma_start(T.sland[me, 96:128, :], T.padr[0:1, :]).then_inc(sem.stst, 16)
+    Y.wait_ge(sem.scq, 1)
+    Y.dma_start(T.sland[me, 0:96, :], T.win1[1:2, 0:T0]).then_inc(sem.stst, 16)
+    Y.wait_ge(sem.valq, N)
+    Y.wait_ge(sem.valo, N)
+    for q in range(4):
+        Y.dma_start(T.val[32 * q + 16:32 * q + 32, :], T.valo[32 * q + 16:32 * q + 32, :]).then_inc(sem.vald, 16)
+
+    for m in range(N):
+        iota(T.val[:, SW * m:SW * m + SW], [[1, SW]], base(plans, m, me) - 200, 0, "valq")
+    g.wait_ge(sem.sto, 1)
+    mst = T.st[:, 8 * me:8 * me + 8]
+    fused([([ranks[d] for d, m in mine["direct"] + mine["near"]], all_mask, "sst", mst, mst)]
+          + [([c], m, "rst_", mst, T.relst[:]) for d, c, m, mo in mine["via"]])
+    land1 = slice(SW * me, SW * me + R1)
+    c1 = (lambda d: T.slot1c[:, Q1 * d:Q1 * d + R1].bitcast(dt.uint8), lambda d: T.land1c[:, land1].bitcast(dt.uint8))
+    s1 = (lambda d: T.slot1s[:, Q1 * d:Q1 * d + R1], lambda d: T.land1s[:, land1])
+    g.wait_ge(sem.pk1c, 1)
+    send_far(c1[0], c1[1], T.rel1c[:].bitcast(dt.uint8), "p1", "r1c")
+    g.wait_ge(sem.pk1s, 1)
+    send_far(s1[0], s1[1], T.rel1s[:], "p1", "r1s")
+    g.wait_ge(sem.stst, 32)
+    fused([([ranks[(me + i) % N] for i in range(1, N)], all_mask, "sls", T.sland[me], T.sland[me])])
+    send_near(c1[0], c1[1], "p1")
+    send_near(s1[0], s1[1], "p1")
+    for m in range(N):
+        iota(T.valo[:, SW * m:SW * m + SW], [[32, 2], [-16, 2], [1, 16]], base(plans, m, me) - 184, 0, "valo")
+
+    w2 = slice(T0 * me, T0 * me + T0 + 32)
+    v(V.memset(T.stf[:, 64:72], float(T0)))
+    v(V.memset(T.c8p[:], 0.0))
+    v(V.memset(T.rst8[:], 1.0))
+    v(V.memset(T.d0[:, 0:64:2], BIG))
+    ts(T.par16[:], T.pi16[:, 0:1], 1.0, None, A.mult)
+    V.wait_ge(sem.gc2, 5)
+    tt(T.kp[:], T.pi15[:], T.k16[:], A.add)
+    vw()
+    v(V.memset(T.rst8[:, 0:64:8], 0.0))
+    ts(T.kt[:], T.fl4[:], T.par1[:], None, A.mult)
+    ts(T.nk[:], T.kp[:], -1.0, None, A.mult)
+    v(V.memset(T.win2[:, w2], 0.0), "w2s")
+    vw()
+    tt(T.kpo[:], T.kp[:], T.kt[:], A.add)
+    V.wait_ge(sem.lw, 16)
+    v(V.quantize_mx(T.qw[:], T.sw[:], T.wt[:]), "qws")
+    vw()
+    ts(T.kpo8[:], T.kpo[:], 8.0, None, A.mult)
+    ts(T.nko8[:], T.kpo[:], -8.0, None, A.mult)
+
+    V.wait_ge(sem.sst, nsl)
+    V.wait_ge(sem.sto, 1)
+    for d in range(N):
+        cp(T.stf[:, 8 * d:8 * d + 8], T.st[:, d:64:8], "stq")
+    V.wait_ge(sem.stq, N)
+    vw()
+    tt(T.nn[:], T.stf[:, 0:64], T.stf[:, 8:72], A.subtract)
+    tt(T.ai[:], T.stf[:, 0:64], T.cA[:], A.add)
+    vw()
+    ts(T.ci[:], T.nn[:], 3, None, A.arith_shift_right)
+    ts(T.ti[:], T.ai[:], 3, None, A.arith_shift_right)
+    vw()
+    cp(T.c8p[:, 1:65], T.ci[:])
+    vw()
+    scan(T.nB[:], T.c8p[:, 0:64], T.rst8[:], A.add, A.mult, "bq")
+    V.wait_ge(sem.bq, 1)
+    tt(T.tq[:], T.ti[:], T.nB[:], A.add)
+    for kk in range(4):
+        ts(T.ge[:, 64 * kk:64 * kk + 64], T.nB[:], T.nk[:, kk:kk + 1], BIG, A.is_ge, A.mult)
+    vw()
+    for kk in range(4):
+        scan(T.sc[:, 64 * kk:64 * kk + 64], T.ge[:, 64 * kk:64 * kk + 64], T.tq[:], A.max, A.min)
+    vw()
+    for kk in range(4):
+        ts(T.off2[:, kk:32:4], T.sc[:, 64 * kk + 7:64 * kk + 64:8], T.kp[:, kk:kk + 1], float(7 * SW + Q1), A.add, A.min, "off2s")
+    S.wait_ge(sem.stq, N)
+    for m in range(N):
+        S.activation(T.stx[:, 8 * m:8 * m + 8], T.stf[:, 8 * me:8 * me + 8], AF.Copy).then_inc(sem.dupq, 1)
+    S.wait_ge(sem.bq, 1)
+    for m in range(N):
+        S.activation(T.nBx[:, 8 * m:8 * m + 8], T.nB[:, 8 * me:8 * me + 8], AF.Identity, float(m), 8.0).then_inc(sem.dupq, 1)
+
+    V.wait_ge(sem.off2s, 4)
+    V.wait_ge(sem.own1c, 1)
+    V.wait_ge(sem.p1, 2 * incoming(every))
+    cp(T.slot2c[:].bitcast(dt.uint32), T.land1c[:].bitcast(dt.uint32).indirect(T.off2[:]), "pk2c")
+    cp(T.land2c[:, 0:OWN].bitcast(dt.uint32), T.land1c[:].bitcast(dt.uint32).indirect(T.off2[:, 4 * me:4 * me + 4]), "own2c")
+    S.wait_ge(sem.off2s, 4)
+    S.wait_ge(sem.p1, 2 * incoming(every))
+    S.wait_ge(sem.own1s, 1)
+    S.activation(T.slot2s[:], T.land1s[:].indirect(T.off2[:]), AF.Copy).then_inc(sem.pk2s, 1)
+    S.activation(T.land2s[:, 0:OWN], T.land1s[:].indirect(T.off2[:, 4 * me:4 * me + 4]), AF.Copy).then_inc(sem.own2s, 1)
+
+    def blk(d):
+        b = base(plans, me, d)
+        return slice(b, b + CAP)
+    c2 = (lambda d: T.slot2c[:, SW * d:SW * d + CAP].bitcast(dt.uint8), lambda d: T.land2c[:, blk(d)].bitcast(dt.uint8))
+    s2 = (lambda d: T.slot2s[:, SW * d:SW * d + CAP], lambda d: T.land2s[:, blk(d)])
+    g.wait_ge(sem.pk2c, 1)
+    send_far(c2[0], c2[1], T.rel2c[:].bitcast(dt.uint8), "p2a", "r2c")
+    g.wait_ge(sem.pk2s, 1)
+    send_far(s2[0], s2[1], T.rel2s[:], "p2a", "r2s")
+    send_near(c2[0], c2[1], "p2a")
+    send_near(s2[0], s2[1], "p2a")
+
+    V.wait_ge(sem.dupq, 2 * N)
+    tt(T.ai2[:], T.stx[:], T.cA2[:], A.add)
+    for kk in range(4):
+        ts(T.ge2[:, 64 * kk:64 * kk + 64], T.nBx[:], T.nko8[:, kk:kk + 1], BIG, A.is_ge, A.mult)
+    vw()
+    ts(T.ti2[:], T.ai2[:], 0xFFF8, None, A.bitwise_and)
+    vw()
+    tt(T.tq2[:], T.ti2[:], T.nBx[:], A.add)
+    vw()
+    for kk in range(4):
+        scan(T.sc2[:, 64 * kk:64 * kk + 64], T.ge2[:, 64 * kk:64 * kk + 64], T.tq2[:], A.max, A.min)
+    vw()
+    for kk in range(4):
+        ts(T.off3[:, kk:32:4], T.sc2[:, 64 * kk + 7:64 * kk + 64:8], T.kpo8[:, kk:kk + 1], 4095.0, A.add, A.min)
+    Y.wait_ge(sem.srz, 6)
+    Y.wait_ge(sem.stst, 32)
+    Y.wait_ge(sem.sls, nsl)
+    for q in range(8):
+        Y.dma_start(T.srow[16 * q:16 * q + 1, :], T.sland[:]).then_inc(sem.srl, 16)
+    V.wait_ge(sem.srl, 128)
+    vw()
+    cp(T.sg2[:], T.srow[:].indirect(T.off3[:]))
+    vw()
+    v(V.transpose(T.tr3[:], T.sg2[:]))
+    vw()
+    for h in range(2):
+        ts(T.d0[:, 2 * h + 1:64:4], T.tr3[:, 16 * h:512:32], float(T0 * me + T0), BIG, A.is_ge, A.mult)
+        cp(T.d1[:, 2 * h:64:4], T.tr3[:, 16 * h:512:32])
+    vw()
+    scan(T.pl[:], T.d0[:], T.d1[:], A.max, A.min)
+    vw()
+    ts(T.off4[:], T.pl[:, 1:64:2], T.par16[:], None, A.add)
+    vw()
+    V.wait_ge(sem.w2s, 1)
+    V.wait_ge(sem.vald, 64)
+    cp(T.win2[:].indirect(T.off4[:]), T.val[:])
+    vw()
+    v(V.transpose(T.tr2[:], T.win2[:, w2]))
+    vw()
+    ts(T.Ie[:], T.tr2[:, 0:416:16], T.epar[:], None, A.mult)
+    ts(T.Io[:], T.tr2[:, 0:416:16], T.par1[:], None, A.mult)
+    vw()
+    tt(T.G2[:, 0:24:2], T.Ie[:, 0:24:2], T.Io[:, 1:24:2], A.add)
+    tt(T.G2[:, 1:24:2], T.Ie[:, 3:26:2], T.Io[:, 0:24:2], A.add)
+    vw()
+    ts(T.off5[:], T.G2[:], 200.0, None, A.add, name="off5s")
+
+    for s_, n_ in (("p2a", 2 * incoming(("direct", "near"))), ("own2c", 1), ("own2s", 1), ("qws", 1)):
+        TE.wait_ge(sem[s_], n_)
+    TE.matmul_mx(T.ps[:, 0:L1], T.qw[:], T.sw[:], T.land2c[:, 0:L1], T.land2s[:, 0:L1], True, True).then_inc(sem.mm0, 1)
+    TE.wait_ge(sem.p2b, 2 * incoming(("via",)))
+    TE.matmul_mx(T.ps[:, 512:640], T.qw[:], T.sw[:], T.land2c[:, L2 - 128:L2], T.land2s[:, L2 - 128:L2], True, True).then_inc(sem.mm1, 1)
+    S.wait_ge(sem.mm0, 1)
+    S.activation(T.ysb[:, 0:L1], T.ps[:, 0:L1], AF.Copy).then_inc(sem.cps, 1)
+    V.wait_ge(sem.mm1, 1)
+    cp(T.ysb[:, L1:L2], T.ps[:, 640 - L2 + L1:640], "cpv")
+    for q in (V, S):
+        q.wait_ge(sem.off5s, 1)
+        q.wait_ge(sem.cpv, 1)
+        q.wait_ge(sem.cps, 1)
+    cp(T.yo[:, 0:192], T.ysb[:].indirect(T.off5[:, 0:12]), "yv")
+    S.activation(T.yo[:, 192:384], T.ysb[:].indirect(T.off5[:, 12:24]), AF.Copy).then_inc(sem.ys, 1)
+    Y.wait_ge(sem.yv, 1)
+    Y.dma_start(T.y[:, 0:192], T.yo[:, 0:192]).then_inc(sem.yst, 16)
+    S.wait_ge(sem.ys, 1)
+    S.dma_start(T.y[:, 192:384], T.yo[:, 192:384]).then_inc(sem.yst, 16)
+    Y.wait_ge(sem.yst, 32)
+    g.wait_ge(sem.loc, ln[0])

@@ -3,11 +3,11 @@ from concourse.mybir import dt, AluOpType as A, ActivationFunctionType as AF
 
 T0, N, Q1, CAP, SW = 384, 8, 48, 56, 64
 R1 = Q1 + 1
-OWN = 64
-L2 = OWN + 7 * CAP
-L1 = L2 - 2 * CAP
-NOPL = 8191.0
+HALF = 4 * Q1 + 16
+L2 = 8 + N * CAP
+EMPTY = -1024
 BIG = 65536.0
+ROUND = 12582912
 X4, U8, U16, F32, BF, I32 = "float8_e4m3fn_x4", "uint8", "uint16", "float32", "bfloat16", "int32"
 
 
@@ -17,33 +17,28 @@ def sb(n, t):
 
 SCRATCH = {
     "xt": sb(1536, BF), "wt": sb(512, BF), "qx": sb(T0, X4), "sx": sb(T0, U8), "qw": sb(128, X4), "sw": sb(128, U8),
-    "slot1c": sb(400, X4), "slot1s": sb(400, U8), "land1c": sb(512, X4), "land1s": sb(512, U8),
-    "slot2c": sb(512, X4), "slot2s": sb(512, U8), "land2c": sb(L2, X4), "land2s": sb(L2, U8),
-    "relst": sb(8, U16), "rel1c": sb(R1, X4), "rel1s": sb(R1, U8), "rel2c": sb(CAP, X4), "rel2s": sb(CAP, U8),
-    "tab": sb(24, I32), "key": sb(24, I32), "tabk": sb(32, F32), "M": sb(192, F32),
-    "W": sb(816, F32), "z192": sb(192, F32), "rst32": sb(32, F32), "rst8": sb(64, F32),
-    "gd": sb(192, F32), "td": sb(192, F32), "pos": sb(192, F32), "trr": sb(32, F32),
-    "torc": sb(T0, F32), "padr": sb(128, F32), "tt0": sb(32, F32),
-    "Qs": sb(32, F32), "tb": sb(96, F32), "tb2": sb(96, F32), "F": sb(8, F32), "off1": sb(24, U16),
-    "win1": sb(512, F32), "tr1": sb(512, F32), "Ge": sb(32, F32), "Go": sb(32, F32), "G": sb(24, F32),
-    "g1": sb(26, U16), "ownl": sb(4, U16), "srow": sb(4096, F32), "zz": sb(768, BF),
-    "pidx": sb(4, I32), "pi15": sb(4, I32), "pi16": sb(4, I32), "par15": sb(1, F32), "par128": sb(1, F32),
-    "par16": sb(1, F32), "par1": sb(1, F32), "epar": sb(1, F32), "k16": sb(4, F32), "fl4": sb(4, F32), "kp": sb(4, F32),
-    "kt": sb(4, F32), "kpo": sb(4, F32), "kpo8": sb(4, F32), "nk": sb(4, F32), "nko8": sb(4, F32), "cA": sb(64, F32),
-    "cA2": sb(64, F32), "st": sb(64, U16), "stf": sb(72, F32), "nn": sb(64, I32), "ai": sb(64, I32), "ci": sb(64, I32),
-    "ti": sb(64, I32), "c8p": sb(66, F32), "nB": sb(64, F32), "ge": sb(256, F32), "tq": sb(64, F32), "sc": sb(256, F32),
-    "off2": sb(32, U16), "nBx": sb(64, F32), "stx": sb(64, F32), "ai2": sb(64, I32), "ti2": sb(64, I32),
-    "tq2": sb(64, F32), "ge2": sb(256, F32), "sc2": sb(256, F32), "off3": sb(32, U16),
-    "sg2": sb(512, F32), "tr3": sb(512, F32), "d0": sb(64, F32), "d1": sb(64, F32), "pl": sb(64, F32), "off4": sb(32, U16),
-    "val": sb(512, BF), "valo": sb(512, BF), "win2": sb(3712, BF), "tr2": sb(416, BF), "Ie": sb(26, F32),
-    "Io": sb(26, F32), "G2": sb(24, F32), "off5": sb(24, U16), "ysb": sb(L2, F32), "yo": sb(T0, F32),
-    "sland": ("dram", [8, 128, 4], F32), "ps": ("psum", [128, 1024], F32),
+    "slot1c": sb(2 * HALF, X4), "slot1s": sb(2 * HALF, U8), "land1c": sb(512, X4), "land1s": sb(512, U8),
+    "slot2c": sb(N * CAP, X4), "slot2s": sb(N * CAP, U8), "land2c": sb(L2, X4), "land2s": sb(L2, U8),
+    "relst": sb(8, U16), "rel1c": sb(Q1 + R1, X4), "rel1s": sb(Q1 + R1, U8), "rel2c": sb(2 * CAP, X4),
+    "rel2s": sb(2 * CAP, U8),
+    "tab": sb(12, I32), "tabk": sb(12, F32), "Lt": sb(108, F32), "C": sb(408, F32), "TT": sb(97, F32), "Sq": sb(64, F32),
+    "F": sb(32, F32), "bc": sb(32, F32), "bct": sb(32, F32), "gd": sb(96, F32), "td": sb(96, F32), "pos": sb(96, F32),
+    "e0": sb(36, F32), "e1": sb(36, F32), "e2": sb(36, F32), "off1": sb(12, U16), "torc": sb(192, BF),
+    "win1": sb(416, BF), "trA": sb(416, BF), "trB": sb(T0, BF), "U": sb(32, F32), "sel": sb(2, U16), "g1": sb(32, U16),
+    "ownl": sb(4, U16), "pidx": sb(4, I32), "pi15": sb(4, I32), "pi16": sb(1, I32), "pi1": sb(1, I32), "pi8": sb(1, I32),
+    "par8": sb(1, F32), "epar": sb(1, F32), "k16": sb(4, F32), "kp": sb(4, F32), "kp8": sb(4, F32), "nk": sb(4, F32),
+    "lo": sb(1, F32), "hi": sb(1, F32), "j23": sb(2, F32), "da": sb(1, F32), "db": sb(1, F32), "dl": sb(1, F32),
+    "selD": sb(2, U16), "stage": sb(26, I32), "offp": sb(12, U16), "pb": sb(192, BF), "prow": sb(192, BF),
+    "e48": sb(48, BF), "win2": sb(N * T0, BF), "X": sb(416, BF), "Xk": sb(416, F32), "Xt": sb(416, F32),
+    "rstD": sb(416, F32), "Xs": sb(416, F32), "t8": sb(8, F32), "kin": sb(32, F32), "kt": sb(32, F32),
+    "cd": sb(32, I32), "mi": sb(24, I32), "ki": sb(24, I32), "mf": sb(24, F32), "sf": sb(24, F32), "off5": sb(24, U16),
+    "cA": sb(64, F32), "cS": sb(64, F32), "st": sb(64, U16), "stf": sb(72, F32), "nn": sb(64, I32), "ai": sb(64, I32),
+    "ci": sb(64, I32), "ti": sb(64, I32), "c8p": sb(66, F32), "rst8": sb(64, F32), "nB": sb(64, F32), "nBs": sb(64, F32),
+    "ge": sb(256, F32), "tq": sb(64, F32), "sc": sb(256, F32), "ma": sb(4, F32), "mb": sb(4, F32), "mc": sb(4, F32),
+    "off2": sb(32, U16), "ownm": sb(4, U16), "ysb": sb(L2, F32), "yo": sb(T0, F32),
+    "pd": ("dram", [8, 128, 6], BF), "lq": ("dram", [8, 128, 6], BF), "ps": ("psum", [128, 1024], F32),
 }
-SEMAPHORES = ["vq", "gc1", "gct", "gc2", "lt", "lx", "lw", "keyq", "ms", "gds", "fs", "tds", "trs", "torw", "sto", "qxs",
-              "g1s", "pk1c", "pk1s", "scq", "owns", "own1c", "own1s", "stst", "srz", "wz", "off2s", "pk2c", "pk2s",
-              "own2c", "own2s", "srl", "mm0", "mm1", "cpv", "cps", "off5s", "yv", "ys", "yst", "qws", "sst", "sls", "p1",
-              "p2a", "p2b", "loc", "zzs", "bq", "stq", "dupq", "valq", "valo", "vald", "w2s", "rst_", "r1c", "r1s", "r2c",
-              "r2s"]
+SEMAPHORES = ["sst", "sls", "p1c", "p1s", "p2c", "p2s", "loc"] + ["s%d" % i for i in range(100)]
 
 
 def bits(m):
@@ -54,49 +49,70 @@ def mask_of(es):
     return sum(1 << x for x in es)
 
 
-def plan(topo, ranks, r):
-    me = ranks[r]
-    order = [(r + i) % N for i in range(1, N)]
-    far = [d for d in order if topo.chip(ranks[d]) != topo.chip(me)]
-    near = [d for d in order if topo.chip(ranks[d]) == topo.chip(me)]
-    hands = [c for c in topo.cores_of(me) if c not in ranks and topo.die(c) == topo.die(me)]
-    e = topo.engines(me, ranks[far[0]])
-    rest = [x for x in topo.engines(me, hands[0]) if x not in e]
-    direct = [(d, mask_of(e[2 * i:2 * i + 2])) for i, d in enumerate(far[:4])]
-    half = len(rest) // 2
-    via = [(d, hands[i], mask_of(rest[half * i:half * i + half]), topo.mask(hands[i], ranks[d]))
-           for i, d in enumerate(far[4:])]
-    return {"direct": direct, "via": via, "near": [(d, mask_of(rest)) for d in near]}
-
-
 def dst_of(topo, c):
     a = topo.addr(c)
     return DstId(rid=a[0], pnc=a[1])
 
 
-def base(plans, s, d):
-    cyc = [(d + k) % N for k in range(1, N)]
-    late = [q for q in cyc if d in [v[0] for v in plans[q]["via"]]]
-    order = [q for q in cyc if q not in late] + late
-    return 0 if s == d else OWN + CAP * order.index(s)
+def plan(topo, ranks, r):
+    me, a = ranks[r], r // 2
+    assert all(topo.chip(ranks[2 * i]) == topo.chip(ranks[2 * i + 1]) for i in range(N // 2))
+
+    def hands(c):
+        return [h for h in topo.cores_of(c) if h not in ranks and topo.die(h) == topo.die(c)]
+    there = [ranks[q] for q in (2 * (a ^ 2), 2 * (a ^ 2) + 1) if topo.die(ranks[q]) == topo.die(me)][0]
+    out = topo.engines(me, there)
+    return {"direct": a ^ 1, "split": a ^ 2, "carried": a ^ 3, "near": r ^ 1, "hc": hands(me)[0], "hs": hands(me)[1],
+            "hf": hands(there)[2], "out": out, "home": [x for x in topo.engines(me, ranks[r ^ 1]) if x not in out]}
+
+
+def halves(es):
+    return mask_of(es[:len(es) // 2]), mask_of(es[len(es) // 2:])
+
+
+def u8(ap):
+    return ap.bitcast(dt.uint8)
+
+
+def u32(ap):
+    return ap.bitcast(dt.uint32)
+
+
+def pair2(s, a):
+    return 2 * a + 1 - s % 2, 2 * a + s % 2
+
+
+def blk2(s, d):
+    b = 8 + CAP * ((s - d) % N)
+    return slice(b, b + CAP)
 
 
 def hand_on(g, core, T, topo, ranks, plans):
     for s in range(N):
-        for d, c, m_in, m_out in plans[s]["via"]:
-            if c != core:
-                continue
-            b = base(plans, s, d)
-            steps = [("rst_", T.relst[:], T.st[:, 8 * s:8 * s + 8], "sst"),
-                     ("r1c", T.rel1c[:].bitcast(dt.uint8), T.land1c[:, SW * s:SW * s + R1].bitcast(dt.uint8), "p1"),
-                     ("r1s", T.rel1s[:], T.land1s[:, SW * s:SW * s + R1], "p1"),
-                     ("r2c", T.rel2c[:].bitcast(dt.uint8), T.land2c[:, b:b + CAP].bitcast(dt.uint8), "p2b"),
-                     ("r2s", T.rel2s[:], T.land2s[:, b:b + CAP], "p2b")]
-            for sem, src, dst, rsem in steps:
-                g.wait_ge(T.sem[sem], bits(m_in))
-                g.remote_dma_fused([RemoteDMATransfer(dst_ids=[dst_of(topo, ranks[d])], dma_engine_mask=m_out,
-                                                      remote_sem=T.sem[rsem], src=src, dst=dst)], local_sem=T.sem.loc)
-            g.wait_ge(T.sem.loc, len(steps) * bits(m_out))
+        p = plans[s]
+        if core not in (p["hc"], p["hs"], p["hf"]):
+            continue
+        a = p["split"] if core == p["hf"] else p["carried"]
+        ms = halves(topo.engines(core, ranks[2 * a]))
+        l1, mst = slice(SW * s, SW * s + R1), T.st[:, 8 * s:8 * s + 8]
+        one, two = (2 * a, 2 * a + 1), pair2(s, a)
+        steps = {
+            "p1c": [(d, ms[y], u8(T.rel1c[:, Q1 * y:Q1 * y + R1]), u8(T.land1c[:, l1])) for y, d in enumerate(one)],
+            "p1s": [(d, ms[y], T.rel1s[:, Q1 * y:Q1 * y + R1], T.land1s[:, l1]) for y, d in enumerate(one)],
+            "p2c": [(d, ms[y], u8(T.rel2c[:, CAP * y:CAP * y + CAP]), u8(T.land2c[:, blk2(s, d)])) for y, d in enumerate(two)],
+            "p2s": [(d, ms[y], T.rel2s[:, CAP * y:CAP * y + CAP], T.land2s[:, blk2(s, d)]) for y, d in enumerate(two)]}
+        if core == p["hf"]:
+            steps["sst"] = [(d, ms[y], T.relst[:], mst) for y, d in enumerate(one)]
+            order, m_in = ["sst", "p1c", "p1s", "p2c", "p2s"], len(p["out"])
+        else:
+            y = 0 if core == p["hc"] else 1
+            steps["sst"] = [(one[y], ms[0] | ms[1], T.relst[:], mst)]
+            order, m_in = ["sst", "p1" + "cs"[y], "p2" + "cs"[y]], len(p["home"])
+        for sem in order:
+            g.wait_ge(T.sem[sem], m_in)
+            g.remote_dma_fused([RemoteDMATransfer(dst_ids=[dst_of(topo, ranks[d])], dma_engine_mask=m, remote_sem=T.sem[sem],
+                                                  src=src, dst=dst) for d, m, src, dst in steps[sem]], local_sem=T.sem.loc)
+        g.wait_ge(T.sem.loc, len(order) * bits(ms[0] | ms[1]))
 
 
 def rank_program(g, core, T, topo):
@@ -106,334 +122,335 @@ def rank_program(g, core, T, topo):
     if me is None:
         hand_on(g, core, T, topo, ranks, plans)
         return
-    V, S, Y, TE, sem = g.vector, g.scalar, g.sync, g.tensor, T.sem
-    vn, ln = [0], [0]
-    mine = plans[me]
+    V, S, Y, TE = g.vector, g.scalar, g.sync, g.tensor
+    mine, par, chip = plans[me], me % 2, me // 2
+    names, count, seen, ln = {}, {}, {}, [0]
 
-    def v(ins, name=None):
-        if name is None:
-            ins.then_inc(sem.vq, 1)
-            vn[0] += 1
-        else:
-            ins.then_inc(sem[name], 1)
+    def inc(ins, name, n=1):
+        names.setdefault(name, T.sem["s%d" % len(names)])
+        ins.then_inc(names[name], n)
+        count[name] = count.get(name, 0) + n
 
-    def vw():
-        V.wait_ge(sem.vq, vn[0])
+    def wait(q, *ns):
+        for name in ns:
+            q.wait_ge(names[name], count[name])
+            seen[name] = count[name]
 
-    def ts(out, in0, s1, s2, o0, o1=None, name=None):
-        v(V.tensor_scalar(out, in0, s1, s2, o0, o1) if o1 is not None else V.tensor_scalar(out, in0, s1, s2, o0), name)
+    def ts(name, out, in0, s1, s2, o0, o1=None):
+        inc(V.tensor_scalar(out, in0, s1, s2, o0, o1) if o1 is not None else V.tensor_scalar(out, in0, s1, s2, o0), name)
 
-    def tt(out, a, b, op, name=None):
-        v(V.tensor_tensor(out, a, b, op), name)
+    def tt(name, out, a, b, op):
+        inc(V.tensor_tensor(out, a, b, op), name)
 
-    def cp(out, in_, name=None):
-        v(V.tensor_copy(out, in_), name)
+    def cp(name, out, in_):
+        inc(V.tensor_copy(out, in_), name)
 
-    def scan(out, a, b, o0, o1, name=None):
-        v(V.tensor_tensor_scan(out, a, b, 0.0, o0, o1), name)
+    def scan(name, out, a, b, init, o0, o1):
+        inc(V.tensor_tensor_scan(out, a, b, init, o0, o1), name)
+
+    def tr(name, out, in_):
+        inc(V.transpose(out, in_), name)
+
+    def fill(name, out, c):
+        inc(V.memset(out, c), name)
+
+    def act(name, out, in_, *bias_scale):
+        inc(S.activation(out, in_, AF.Identity if bias_scale else AF.Copy, *bias_scale), name)
+
+    def dma(q, name, out, in_):
+        inc(q.dma_start(out, in_), name, 16)
+
+    def iota(name, out, pat, b, cm=0):
+        inc(g.iota(out, pat, b, cm, allow_small_or_imprecise_dtypes=True), name)
 
     def fused(trs):
-        g.remote_dma_fused([RemoteDMATransfer(dst_ids=[dst_of(topo, c) for c in cs], dma_engine_mask=m, remote_sem=sem[rs],
-                                              srcs=[s], dsts=[d for c in cs]) for cs, m, rs, s, d in trs], local_sem=sem.loc)
-        ln[0] += sum(bits(t[1]) for t in trs)
+        g.remote_dma_fused([RemoteDMATransfer(dst_ids=[dst_of(topo, c) for c, d in to], dma_engine_mask=m,
+                                              remote_sem=T.sem[rs], srcs=[s], dsts=[d for c, d in to])
+                            for m, rs, s, to in trs], local_sem=T.sem.loc)
+        ln[0] += sum(bits(t[0]) for t in trs)
 
-    def send_far(src, dst, rel, rsem, relsem):
-        fused([([ranks[d]], m, rsem, src(d), dst(d)) for d, m in mine["direct"]]
-              + [([c], m, relsem, src(d), rel) for d, c, m, mo in mine["via"]])
+    out, home = mask_of(mine["out"]), mask_of(mine["home"])
+    outs = halves(mine["out"])
+    n_in = 2 * bits(outs[0]) + bits(home) + (bits(out) + bits(home)) + 2 * bits(outs[0])
+    n_st = 2 * bits(out) + bits(home) + (bits(out) + bits(home)) + 2 * bits(out)
 
-    def send_near(src, dst, rsem):
-        fused([([ranks[d]], m, rsem, src(d), dst(d)) for d, m in mine["near"]])
-
-    def incoming(kinds):
-        return sum(bits(t[-1]) for r in range(N) for k in kinds for t in plans[r][k] if t[0] == me)
-    every = ("direct", "near", "via")
-
-    all_mask = topo.mask(core, ranks[mine["direct"][0][0]])
-    nsl = bits(all_mask) * (N - 1)
-
-    for q in range(8):
-        (Y if q % 2 == 0 else S).dma_start(T.tab[16 * q:16 * q + 16, :], T.to[:]).then_inc(sem.lt, 16)
-    S.dma_start(T.xt[:], T.x[:]).then_inc(sem.lx, 16)
-
-    def iota(out, pat, b, cm, s):
-        g.iota(out, pat, b, cm, allow_small_or_imprecise_dtypes=True).then_inc(sem[s], 1)
-    g.iota(T.pidx[:], [[0, 4]], 0, 1).then_inc(sem.gc1, 1)
-    iota(T.torc[:], [[1, T0]], 0, 0, "gct")
-    iota(T.k16[:], [[16, 4]], 0, 0, "gc2")
-    iota(T.fl4[:], [[0, 2], [-32, 2]], 16, 0, "gc2")
-    iota(T.cA[:], [[0, 8], [512, 8]], 7 - me, 0, "gc2")
-    iota(T.cA2[:], [[-1, 8], [512, 8]], 7, 0, "gc2")
-    iota(T.d1[:, 1:64:2], [[16, 32]], N * T0, 1, "gc2")
-
-    v(V.memset(T.zz[:], 0.0), "zzs")
-    v(V.memset(T.padr[:], NOPL), "wz")
-    v(V.memset(T.W[:, 23:791:24], 0.0))
-    v(V.memset(T.tabk[:], 0.0))
-    v(V.memset(T.z192[:], 0.0))
-    v(V.memset(T.rst32[:], 1.0))
-    v(V.memset(T.g1[:], 0))
-    v(V.memset(T.ownl[:], 0))
-    V.wait_ge(sem.gc1, 1)
-    ts(T.pi15[:], T.pidx[:], 15, None, A.bitwise_and)
-    ts(T.pi16[:], T.pidx[:], 16, None, A.bitwise_and)
-    vw()
-    v(V.memset(T.rst32[:, 0:32:16], 0.0))
-    ts(T.par128[:], T.pi16[:, 0:1], 8.0, -1.0, A.mult, A.add)
-    ts(T.par1[:], T.pi16[:, 0:1], 0.0625, None, A.mult)
-    ts(T.epar[:], T.pi16[:, 0:1], -0.0625, 1.0, A.mult, A.add)
-    v(V.memset(T.win1[:], 0.0))
-    S.wait_ge(sem.zzs, 1)
-    for h in range(2):
-        S.activation(T.srow[:, 768 * h:768 * h + 768], T.zz[:], AF.Copy).then_inc(sem.srz, 1)
-
-    vw()
-    V.wait_ge(sem.lt, 128)
-    cp(T.tabk[:, 0:24], T.tab[:], "gds")
-    ts(T.key[:], T.tab[:], 1.0 / T0, 0.5 / T0 - 0.5, A.mult, A.add, name="keyq")
-    V.wait_ge(sem.gds, 1)
-    v(V.transpose(T.trr[:], T.tabk[:]), "trs")
-    V.wait_ge(sem.keyq, 1)
-    for d in range(N):
-        ts(T.M[:, 24 * d:24 * d + 24], T.key[:], float(d), None, A.is_equal, name="ms")
-    Y.wait_ge(sem.trs, 1)
-    Y.wait_ge(sem.gct, 1)
-    Y.dma_start(T.torc[1:2, :], T.trr[0:24, 0:16]).then_inc(sem.torw, 16)
-    Y.dma_start(T.wt[:], T.w[:]).then_inc(sem.lw, 16)
-    V.wait_ge(sem.ms, N)
-    scan(T.W[:, 24:216], T.M[:], T.z192[:], A.add, A.add)
-    S.wait_ge(sem.gds, 1)
-    for d in range(N):
-        S.activation(T.gd[:, d:192:8], T.tabk[:, 0:24], AF.Identity, 512.0 - 1024.0 * T0 * d, 1024.0).then_inc(sem.gds, 1)
-    vw()
-    v(V.transpose(T.tt0[:], T.W[:, 23:791:24]))
-    vw()
-    scan(T.Qs[:], T.rst32[:], T.tt0[:], A.mult, A.add)
-    vw()
-    ts(T.tb[:, 0:32], T.Qs[:], -1.0, T.Qs[:, 15:16], A.mult, A.add)
-    tt(T.tb[:, 32:64], T.Qs[:], T.tt0[:], A.subtract)
-    vw()
-    v(V.transpose(T.tb2[:, 0:64], T.tb[:, 0:64]))
-    ts(T.tb[:, 64:96], T.Qs[:], 0.0, T.Qs[:, 15:16], A.mult, A.add)
-    vw()
-    tt(T.F[:], T.tb2[:, 0:8], T.tb2[:, 33:41], A.add, "fs")
-    v(V.transpose(T.tb2[:, 64:96], T.tb[:, 64:96]))
-    V.wait_ge(sem.fs, 1)
-    S.wait_ge(sem.fs, 1)
-    for d in range(5):
-        ts(T.td[:, d:192:8], T.W[:, 24 + 24 * d:48 + 24 * d], T.F[:, d:d + 1], None, A.add)
-    for d in range(5, N):
-        S.activation(T.td[:, d:192:8], T.W[:, 24 + 24 * d:48 + 24 * d], AF.Identity, T.F[:, d:d + 1]).then_inc(sem.tds, 1)
-    vw()
-    cp(T.st[:, 8 * me:8 * me + 8], T.tb2[:, 64:72], "sto")
-    V.wait_ge(sem.tds, N - 5)
-    V.wait_ge(sem.gds, N + 1)
-    scan(T.pos[:], T.gd[:], T.td[:], A.max, A.min)
-    vw()
-    ts(T.off1[:], T.pos[:, 7:192:8], T.par128[:], None, A.add)
-    V.wait_ge(sem.gct, 1)
-    V.wait_ge(sem.torw, 16)
-    vw()
-    cp(T.win1[:].indirect(T.off1[:, 0:24]), T.torc[:], "scq")
-    V.wait_ge(sem.lx, 16)
-    v(V.quantize_mx(T.qx[:], T.sx[:], T.xt[:]), "qxs")
-    V.wait_ge(sem.scq, 1)
-    for m in range(N):
-        v(V.transpose(T.tr1[:, 64 * m:64 * m + 64], T.win1[:, m:512:8]))
-    vw()
-    ts(T.Ge[:], T.tr1[:, 0:512:16], T.epar[:], None, A.mult)
-    ts(T.Go[:], T.tr1[:, 0:512:16], T.par1[:], None, A.mult)
-    vw()
-    tt(T.G[:, 0:24:3], T.Ge[:, 0:32:4], T.Go[:, 1:32:4], A.add)
-    tt(T.G[:, 1:24:3], T.Ge[:, 3:32:4], T.Go[:, 0:32:4], A.add)
-    tt(T.G[:, 2:24:3], T.Ge[:, 2:32:4], T.Go[:, 3:32:4], A.add)
-    vw()
-    cp(T.g1[:, 0:24], T.G[:], "g1s")
-    cp(T.ownl[:, 0:3], T.G[:, 3 * me:3 * me + 3], "owns")
-    V.wait_ge(sem.g1s, 1)
-    V.wait_ge(sem.qxs, 1)
-    cp(T.slot1c[:].bitcast(dt.uint32), T.qx[:].bitcast(dt.uint32).indirect(T.g1[:, 0:25]), "pk1c")
-    for h in range(2, 4):
-        S.activation(T.srow[:, 768 * h:768 * h + 768], T.zz[:], AF.Copy).then_inc(sem.srz, 1)
-    S.wait_ge(sem.g1s, 1)
-    S.wait_ge(sem.qxs, 1)
-    S.activation(T.slot1s[:], T.sx[:].indirect(T.g1[:, 0:25]), AF.Copy).then_inc(sem.pk1s, 1)
-    V.wait_ge(sem.owns, 1)
-    own1 = slice(SW * me, SW * me + SW)
-    cp(T.land1c[:, own1].bitcast(dt.uint32), T.qx[:].bitcast(dt.uint32).indirect(T.ownl[:]), "own1c")
-    S.wait_ge(sem.owns, 1)
-    S.activation(T.land1s[:, own1], T.sx[:].indirect(T.ownl[:]), AF.Copy).then_inc(sem.own1s, 1)
-    for lo, hi in ((3072, 3840), (3840, 4096)):
-        S.activation(T.srow[:, lo:hi], T.zz[:, 0:hi - lo], AF.Copy).then_inc(sem.srz, 1)
-    Y.wait_ge(sem.wz, 1)
-    Y.dma_start(T.sland[me, 96:128, :], T.padr[0:1, :]).then_inc(sem.stst, 16)
-    Y.wait_ge(sem.scq, 1)
-    Y.dma_start(T.sland[me, 0:96, :], T.win1[1:2, 0:T0]).then_inc(sem.stst, 16)
-    Y.wait_ge(sem.valq, N)
-    Y.wait_ge(sem.valo, N)
     for q in range(4):
-        Y.dma_start(T.val[32 * q + 16:32 * q + 32, :], T.valo[32 * q + 16:32 * q + 32, :]).then_inc(sem.vald, 16)
+        dma(Y if q % 2 == 0 else S, "tab", T.tab[32 * q:32 * q + 32, :], T.to[:])
+    dma(S, "x", T.xt[:], T.x[:])
 
-    for m in range(N):
-        iota(T.val[:, SW * m:SW * m + SW], [[1, SW]], base(plans, m, me) - 200, 0, "valq")
-    g.wait_ge(sem.sto, 1)
-    mst = T.st[:, 8 * me:8 * me + 8]
-    fused([([ranks[d] for d, m in mine["direct"] + mine["near"]], all_mask, "sst", mst, mst)]
-          + [([c], m, "rst_", mst, T.relst[:]) for d, c, m, mo in mine["via"]])
-    land1 = slice(SW * me, SW * me + R1)
-    c1 = (lambda d: T.slot1c[:, Q1 * d:Q1 * d + R1].bitcast(dt.uint8), lambda d: T.land1c[:, land1].bitcast(dt.uint8))
-    s1 = (lambda d: T.slot1s[:, Q1 * d:Q1 * d + R1], lambda d: T.land1s[:, land1])
-    g.wait_ge(sem.pk1c, 1)
-    send_far(c1[0], c1[1], T.rel1c[:].bitcast(dt.uint8), "p1", "r1c")
-    g.wait_ge(sem.pk1s, 1)
-    send_far(s1[0], s1[1], T.rel1s[:], "p1", "r1s")
-    g.wait_ge(sem.stst, 32)
-    fused([([ranks[(me + i) % N] for i in range(1, N)], all_mask, "sls", T.sland[me], T.sland[me])])
-    send_near(c1[0], c1[1], "p1")
-    send_near(s1[0], s1[1], "p1")
-    for m in range(N):
-        iota(T.valo[:, SW * m:SW * m + SW], [[32, 2], [-16, 2], [1, 16]], base(plans, m, me) - 184, 0, "valo")
-
-    w2 = slice(T0 * me, T0 * me + T0 + 32)
-    v(V.memset(T.stf[:, 64:72], float(T0)))
-    v(V.memset(T.c8p[:], 0.0))
-    v(V.memset(T.rst8[:], 1.0))
-    v(V.memset(T.d0[:, 0:64:2], BIG))
-    ts(T.par16[:], T.pi16[:, 0:1], 1.0, None, A.mult)
-    V.wait_ge(sem.gc2, 5)
-    tt(T.kp[:], T.pi15[:], T.k16[:], A.add)
-    vw()
-    v(V.memset(T.rst8[:, 0:64:8], 0.0))
-    ts(T.kt[:], T.fl4[:], T.par1[:], None, A.mult)
-    ts(T.nk[:], T.kp[:], -1.0, None, A.mult)
-    v(V.memset(T.win2[:, w2], 0.0), "w2s")
-    vw()
-    tt(T.kpo[:], T.kp[:], T.kt[:], A.add)
-    V.wait_ge(sem.lw, 16)
-    v(V.quantize_mx(T.qw[:], T.sw[:], T.wt[:]), "qws")
-    vw()
-    ts(T.kpo8[:], T.kpo[:], 8.0, None, A.mult)
-    ts(T.nko8[:], T.kpo[:], -8.0, None, A.mult)
-
-    V.wait_ge(sem.sst, nsl)
-    V.wait_ge(sem.sto, 1)
-    for d in range(N):
-        cp(T.stf[:, 8 * d:8 * d + 8], T.st[:, d:64:8], "stq")
-    V.wait_ge(sem.stq, N)
-    vw()
-    tt(T.nn[:], T.stf[:, 0:64], T.stf[:, 8:72], A.subtract)
-    tt(T.ai[:], T.stf[:, 0:64], T.cA[:], A.add)
-    vw()
-    ts(T.ci[:], T.nn[:], 3, None, A.arith_shift_right)
-    ts(T.ti[:], T.ai[:], 3, None, A.arith_shift_right)
-    vw()
-    cp(T.c8p[:, 1:65], T.ci[:])
-    vw()
-    scan(T.nB[:], T.c8p[:, 0:64], T.rst8[:], A.add, A.mult, "bq")
-    V.wait_ge(sem.bq, 1)
-    tt(T.tq[:], T.ti[:], T.nB[:], A.add)
-    for kk in range(4):
-        ts(T.ge[:, 64 * kk:64 * kk + 64], T.nB[:], T.nk[:, kk:kk + 1], BIG, A.is_ge, A.mult)
-    vw()
-    for kk in range(4):
-        scan(T.sc[:, 64 * kk:64 * kk + 64], T.ge[:, 64 * kk:64 * kk + 64], T.tq[:], A.max, A.min)
-    vw()
-    for kk in range(4):
-        ts(T.off2[:, kk:32:4], T.sc[:, 64 * kk + 7:64 * kk + 64:8], T.kp[:, kk:kk + 1], float(7 * SW + Q1), A.add, A.min, "off2s")
-    S.wait_ge(sem.stq, N)
-    for m in range(N):
-        S.activation(T.stx[:, 8 * m:8 * m + 8], T.stf[:, 8 * me:8 * me + 8], AF.Copy).then_inc(sem.dupq, 1)
-    S.wait_ge(sem.bq, 1)
-    for m in range(N):
-        S.activation(T.nBx[:, 8 * m:8 * m + 8], T.nB[:, 8 * me:8 * me + 8], AF.Identity, float(m), 8.0).then_inc(sem.dupq, 1)
-
-    V.wait_ge(sem.off2s, 4)
-    V.wait_ge(sem.own1c, 1)
-    V.wait_ge(sem.p1, 2 * incoming(every))
-    cp(T.slot2c[:].bitcast(dt.uint32), T.land1c[:].bitcast(dt.uint32).indirect(T.off2[:]), "pk2c")
-    cp(T.land2c[:, 0:OWN].bitcast(dt.uint32), T.land1c[:].bitcast(dt.uint32).indirect(T.off2[:, 4 * me:4 * me + 4]), "own2c")
-    S.wait_ge(sem.off2s, 4)
-    S.wait_ge(sem.p1, 2 * incoming(every))
-    S.wait_ge(sem.own1s, 1)
-    S.activation(T.slot2s[:], T.land1s[:].indirect(T.off2[:]), AF.Copy).then_inc(sem.pk2s, 1)
-    S.activation(T.land2s[:, 0:OWN], T.land1s[:].indirect(T.off2[:, 4 * me:4 * me + 4]), AF.Copy).then_inc(sem.own2s, 1)
-
-    def blk(d):
-        b = base(plans, me, d)
-        return slice(b, b + CAP)
-    c2 = (lambda d: T.slot2c[:, SW * d:SW * d + CAP].bitcast(dt.uint8), lambda d: T.land2c[:, blk(d)].bitcast(dt.uint8))
-    s2 = (lambda d: T.slot2s[:, SW * d:SW * d + CAP], lambda d: T.land2s[:, blk(d)])
-    g.wait_ge(sem.pk2c, 1)
-    send_far(c2[0], c2[1], T.rel2c[:].bitcast(dt.uint8), "p2a", "r2c")
-    g.wait_ge(sem.pk2s, 1)
-    send_far(s2[0], s2[1], T.rel2s[:], "p2a", "r2s")
-    send_near(c2[0], c2[1], "p2a")
-    send_near(s2[0], s2[1], "p2a")
-
-    V.wait_ge(sem.dupq, 2 * N)
-    tt(T.ai2[:], T.stx[:], T.cA2[:], A.add)
-    for kk in range(4):
-        ts(T.ge2[:, 64 * kk:64 * kk + 64], T.nBx[:], T.nko8[:, kk:kk + 1], BIG, A.is_ge, A.mult)
-    vw()
-    ts(T.ti2[:], T.ai2[:], 0xFFF8, None, A.bitwise_and)
-    vw()
-    tt(T.tq2[:], T.ti2[:], T.nBx[:], A.add)
-    vw()
-    for kk in range(4):
-        scan(T.sc2[:, 64 * kk:64 * kk + 64], T.ge2[:, 64 * kk:64 * kk + 64], T.tq2[:], A.max, A.min)
-    vw()
-    for kk in range(4):
-        ts(T.off3[:, kk:32:4], T.sc2[:, 64 * kk + 7:64 * kk + 64:8], T.kpo8[:, kk:kk + 1], 4095.0, A.add, A.min)
-    Y.wait_ge(sem.srz, 6)
-    Y.wait_ge(sem.stst, 32)
-    Y.wait_ge(sem.sls, nsl)
-    for q in range(8):
-        Y.dma_start(T.srow[16 * q:16 * q + 1, :], T.sland[:]).then_inc(sem.srl, 16)
-    V.wait_ge(sem.srl, 128)
-    vw()
-    cp(T.sg2[:], T.srow[:].indirect(T.off3[:]))
-    vw()
-    v(V.transpose(T.tr3[:], T.sg2[:]))
-    vw()
+    iota("pidx", T.pidx[:], [[0, 4]], 0, 1)
+    iota("pidx", T.k16[:], [[16, 4]], 0)
+    iota("torc0", T.torc[:], [[16, 12], [1, 8], [192, 2]], -192)
+    iota("e", T.e0[:, 0:36:3], [[0, 12]], 0)
+    iota("e", T.e0[:, 1:36:3], [[0, 12]], 1)
+    iota("e", T.e0[:, 2:36:3], [[0, 12]], 1 - T0)
+    iota("e", T.e1[:, 1:36:3], [[0, 12]], -ROUND)
+    iota("e48", T.e48[:], [[0, 48]], EMPTY)
+    iota("stage0", T.stage[:], [[1, 26]], 0, 24)
+    wait(Y, "stage0")
     for h in range(2):
-        ts(T.d0[:, 2 * h + 1:64:4], T.tr3[:, 16 * h:512:32], float(T0 * me + T0), BIG, A.is_ge, A.mult)
-        cp(T.d1[:, 2 * h:64:4], T.tr3[:, 16 * h:512:32])
-    vw()
-    scan(T.pl[:], T.d0[:], T.d1[:], A.max, A.min)
-    vw()
-    ts(T.off4[:], T.pl[:, 1:64:2], T.par16[:], None, A.add)
-    vw()
-    V.wait_ge(sem.w2s, 1)
-    V.wait_ge(sem.vald, 64)
-    cp(T.win2[:].indirect(T.off4[:]), T.val[:])
-    vw()
-    v(V.transpose(T.tr2[:], T.win2[:, w2]))
-    vw()
-    ts(T.Ie[:], T.tr2[:, 0:416:16], T.epar[:], None, A.mult)
-    ts(T.Io[:], T.tr2[:, 0:416:16], T.par1[:], None, A.mult)
-    vw()
-    tt(T.G2[:, 0:24:2], T.Ie[:, 0:24:2], T.Io[:, 1:24:2], A.add)
-    tt(T.G2[:, 1:24:2], T.Ie[:, 3:26:2], T.Io[:, 0:24:2], A.add)
-    vw()
-    ts(T.off5[:], T.G2[:], 200.0, None, A.add, name="off5s")
+        for e in range(2):
+            dma(Y, "stage", T.stage[16 * h:16 * h + 16, 1 - h + 12 * e:13 - h + 12 * e], T.to[8 * e:8 * e + 8, :])
+    iota("cA", T.cA[:], [[0, 4], [64 - 128 * par, 2], [8 * SW, 8]], 7 - me + 64 * par)
+    iota("cA", T.cS[:], [[0, 4], [8 - 16 * par, 2], [0, 8]], 8 * par - 8)
+    iota("pb0", T.pb[:], [[0, 192]], 0)
+    fill("k0", T.C[:, 11:408:12], 0.0)
+    fill("k0", T.Lt[:, 0:12], 0.0)
+    fill("k0", T.Lt[:, 96:108], 1.0)
+    fill("k0", T.TT[:, 0:65], 0.0)
+    fill("k0", T.win1[:], 0.0)
+    wait(V, "pidx")
+    ts("k1", T.pi15[:], T.pidx[:], 15, None, A.bitwise_and)
+    ts("k1", T.pi16[:], T.pidx[:, 0:1], 16, None, A.bitwise_and)
+    wait(V, "k1")
+    ts("par8", T.par8[:], T.pi16[:], 0.5, None, A.mult)
+    ts("k2", T.epar[:], T.pi16[:], -0.0625, 1.0, A.mult, A.add)
+    tt("k2", T.kp[:], T.pi15[:], T.k16[:], A.add)
+    wait(V, "k2")
+    ts("sel", T.sel[:], T.kp[:, 0:2], 23.0, T.epar[:], A.min, A.add)
+    wait(S, "par8", "torc0")
+    act("torc", T.torc[:], T.torc[:], T.par8[:])
+    wait(Y, "e48")
+    for h in range(2):
+        dma(Y, "win2", T.win2[16 * h:16 * h + 1, :], T.e48[64 * h:64 * h + 64, :])
+    dma(Y, "w", T.wt[:], T.w[:])
 
-    for s_, n_ in (("p2a", 2 * incoming(("direct", "near"))), ("own2c", 1), ("own2s", 1), ("qws", 1)):
-        TE.wait_ge(sem[s_], n_)
-    TE.matmul_mx(T.ps[:, 0:L1], T.qw[:], T.sw[:], T.land2c[:, 0:L1], T.land2s[:, 0:L1], True, True).then_inc(sem.mm0, 1)
-    TE.wait_ge(sem.p2b, 2 * incoming(("via",)))
-    TE.matmul_mx(T.ps[:, 512:640], T.qw[:], T.sw[:], T.land2c[:, L2 - 128:L2], T.land2s[:, L2 - 128:L2], True, True).then_inc(sem.mm1, 1)
-    S.wait_ge(sem.mm0, 1)
-    S.activation(T.ysb[:, 0:L1], T.ps[:, 0:L1], AF.Copy).then_inc(sem.cps, 1)
-    V.wait_ge(sem.mm1, 1)
-    cp(T.ysb[:, L1:L2], T.ps[:, 640 - L2 + L1:640], "cpv")
-    for q in (V, S):
-        q.wait_ge(sem.off5s, 1)
-        q.wait_ge(sem.cpv, 1)
-        q.wait_ge(sem.cps, 1)
-    cp(T.yo[:, 0:192], T.ysb[:].indirect(T.off5[:, 0:12]), "yv")
-    S.activation(T.yo[:, 192:384], T.ysb[:].indirect(T.off5[:, 12:24]), AF.Copy).then_inc(sem.ys, 1)
-    Y.wait_ge(sem.yv, 1)
-    Y.dma_start(T.y[:, 0:192], T.yo[:, 0:192]).then_inc(sem.yst, 16)
-    S.wait_ge(sem.ys, 1)
-    S.dma_start(T.y[:, 192:384], T.yo[:, 192:384]).then_inc(sem.yst, 16)
-    Y.wait_ge(sem.yst, 32)
-    g.wait_ge(sem.loc, ln[0])
+    wait(V, "tab")
+    for d in range(1, N):
+        ts("Lt", T.Lt[:, 12 * d:12 * d + 12], T.tab[:], float(T0 * d), None, A.is_lt)
+    cp("tabk", T.tabk[:], T.tab[:])
+    wait(V, "k0", "Lt")
+    scan("C", T.C[:, 12:108], T.Lt[:, 12:108], T.Lt[:, 0:96], 0.0, A.add, A.subtract)
+    wait(S, "tabk")
+    for d in range(N):
+        act("gd", T.gd[:, d:96:8], T.tabk[:], 512.0 - 1024.0 * T0 * d, 1024.0)
+    wait(V, "C")
+    tr("TT", T.TT[:, 32:64], T.C[:, 11:395:12])
+    tr("TT", T.TT[:, 65:97], T.C[:, 23:407:12])
+    wait(V, "TT")
+    scan("Sq", T.Sq[:], T.TT[:, 32:96], T.TT[:, 0:64], -4.5, A.add, A.subtract)
+    wait(V, "Sq")
+    tr("F", T.F[:], T.Sq[:, 32:64])
+    ts("bc", T.bc[:], T.Sq[:, 0:32], 0.0, T.Sq[:, 31:32], A.mult, A.add)
+    wait(V, "F")
+    wait(S, "F")
+    for d in range(5):
+        ts("td", T.td[:, d:96:8], T.C[:, 12 + 12 * d:24 + 12 * d], T.F[:, d:d + 1], None, A.add)
+    for d in range(5, N):
+        act("td", T.td[:, d:96:8], T.C[:, 12 + 12 * d:24 + 12 * d], T.F[:, d:d + 1])
+    wait(V, "bc")
+    tr("bct", T.bct[:], T.bc[:])
+    wait(V, "td", "gd")
+    scan("pos", T.pos[:], T.gd[:], T.td[:], 0.0, A.max, A.min)
+    wait(V, "bct")
+    mst = T.st[:, 8 * me:8 * me + 8]
+    ts("sto", mst, T.bct[:, 0:8], 4.5, None, A.add)
+    pos = T.pos[:, 7:96:8]
+    wait(V, "pos")
+    ts("qa", T.e1[:, 0:36:3], pos, 0.125, float(ROUND), A.mult, A.add)
+    ts("qa", T.e1[:, 2:36:3], pos, 48.0, 184.0, A.mult, A.add)
+    wait(V, "qa", "e")
+    scan("e2", T.e2[:], T.e0[:], T.e1[:], 0.0, A.mult, A.add)
+    wait(V, "e2")
+    cp("off1", T.off1[:], T.e2[:, 2:36:3])
+    wait(V, "off1", "torc")
+    cp("win1", T.win1[:].indirect(T.off1[:]), T.torc[:])
+    wait(V, "x")
+    inc(V.quantize_mx(T.qx[:], T.sx[:], T.xt[:]), "qx")
+    wait(V, "win1")
+    tr("trA", T.trA[:], T.win1[:])
+    tr("trB", T.trB[:], T.win1[:, 16:400])
+    wait(V, "trA")
+    tt("U", T.U[:, 0:25:2], T.trA[:, 0:416:32], T.trA[:, 16:416:32], A.add)
+    wait(V, "trB")
+    tt("U", T.U[:, 1:25:2], T.trB[:, 0:T0:32], T.trB[:, 16:T0:32], A.add)
+    wait(V, "U", "sel")
+    ts("g1", T.g1[:], T.U[:, 0:25].indirect(T.sel[:]), 192.0, None, A.add)
+    wait(V, "g1", "qx")
+    wait(S, "g1", "qx")
+    own1 = slice(SW * me, SW * me + SW)
+    for i, h in enumerate((mine["split"] // 2, chip // 2)):
+        lst, cols = T.g1[:, 12 * h:12 * h + 13], slice(HALF * h, HALF * h + HALF)
+        cp("pk1c%d" % i, u32(T.slot1c[:, cols]), u32(T.qx[:]).indirect(lst))
+        act("pk1s%d" % i, T.slot1s[:, cols], T.sx[:].indirect(lst))
+    cp("ownl", T.ownl[:], T.g1[:, 3 * me:3 * me + 4])
+    wait(V, "pb0")
+    ts("pb", T.pb[:, 0:192:16], pos, -188.5, None, A.add)
+    wait(V, "ownl")
+    cp("own1c", u32(T.land1c[:, own1]), u32(T.qx[:]).indirect(T.ownl[:]))
+    wait(S, "ownl")
+    act("own1s", T.land1s[:, own1], T.sx[:].indirect(T.ownl[:]))
+
+    def send(ph, pair, single, land, rel):
+        for k in "cs":
+            wait(g, "pk%d%s0" % (ph, k))
+            fused([(out, "p%d%s" % (ph, k), pair(k, mine["split"]), [(mine["hf"], rel(k))]),
+                   (home, "p%d%s" % (ph, k), pair(k, mine["carried"]), [(mine["h" + k], rel(k))])])
+        for k in "cs":
+            wait(g, "pk%d%s1" % (ph, k))
+            fused([(outs[y], "p%d%s" % (ph, k), single(k, d), [(ranks[d], land(k, d))])
+                   for y, d in enumerate((2 * mine["direct"], 2 * mine["direct"] + 1))]
+                  + [(home, "p%d%s" % (ph, k), single(k, mine["near"]), [(ranks[mine["near"]], land(k, mine["near"]))])])
+
+    def view(c, s):
+        return lambda k, cols: u8(c[:, cols]) if k == "c" else s[:, cols]
+    wait(g, "sto")
+    fused([(out, "sst", mst, [(mine["hf"], T.relst[:])] + [(ranks[2 * mine["direct"] + y], mst) for y in range(2)]),
+           (home, "sst", mst, [(mine["hc"], T.relst[:]), (mine["hs"], T.relst[:]), (ranks[mine["near"]], mst)])])
+    v1, w1, r1 = view(T.slot1c, T.slot1s), view(T.land1c, T.land1s), view(T.rel1c, T.rel1s)
+
+    def at1(d):
+        return HALF * (d // 4) + Q1 * (d % 4)
+    send(1, lambda k, a: v1(k, slice(at1(2 * a), at1(2 * a) + Q1 + R1)), lambda k, d: v1(k, slice(at1(d), at1(d) + R1)),
+         lambda k, d: w1(k, slice(SW * me, SW * me + R1)), lambda k: r1(k, slice(0, Q1 + R1)))
+    iota("X0", T.X[:], [[0, 416]], EMPTY)
+    iota("rst0", T.rstD[:], [[0, 416]], 0)
+    wait(g, "rst0")
+    iota("rstD", T.rstD[:, 0:416:16], [[0, 26]], -ROUND)
+
+    wait(V, "pb")
+    tr("prow", T.prow[:], T.pb[:])
+    wait(V, "stage")
+    for e in range(2):
+        cp("offp", T.offp[:, e:12:2], T.stage[:, 12 * e + 1:12 * e + 13:2])
+    wait(V, "prow", "offp", "win2")
+    cp("places", T.win2[:].indirect(T.offp[:]), T.prow[:])
+    wait(Y, "places")
+    for h in range(2):
+        dma(Y, "pd", T.pd[:, 64 * h:64 * h + 64, :], T.win2[16 * h:16 * h + 1, :])
+    for h in range(2):
+        dma(Y, "lq", T.lq[me, 64 * h:64 * h + 64, :], T.win2[16 * h:16 * h + 1, T0 * me:T0 * me + T0])
+    wait(g, "pd")
+    far = [d for d in range(N) if d // 2 != chip]
+    fused([(1 << mine["out"][i], "sls", T.pd[d], [(ranks[d], T.lq[me])]) for i, d in enumerate(far)]
+          + [(1 << mine["home"][0], "sls", T.pd[mine["near"]], [(ranks[mine["near"]], T.lq[me])])])
+    Y.wait_ge(T.sem.sls, N - 1)
+    wait(Y, "lq", "X0")
+    for q in range(8):
+        dma(Y, "X", T.X[16 * q:16 * q + 16, 16 * (q % 2):16 * (q % 2) + T0], T.lq[:])
+
+    fill("k3", T.stf[:, 64:72], float(T0))
+    fill("k3", T.c8p[:, 0:1], 0.0)
+    fill("k3", T.rst8[:], 1.0)
+    ts("k3", T.pi8[:], T.pidx[:, 0:1], 8, None, A.bitwise_and)
+    ts("k3", T.pi1[:], T.pidx[:, 0:1], 1, None, A.bitwise_and)
+    ts("k3", T.kp8[:], T.kp[:], -8.0, None, A.add)
+    ts("k3", T.nk[:], T.kp[:], -1.0, None, A.mult)
+    V.wait_ge(T.sem.sst, n_st)
+    wait(V, "sto")
+    for d in range(N):
+        cp("k3", T.stf[:, 8 * d:8 * d + 8], T.st[:, d:64:8])
+    wait(V, "k3", "cA")
+    tt("l1", T.nn[:], T.stf[:, 0:64], T.stf[:, 8:72], A.subtract)
+    tt("l1", T.ai[:], T.stf[:, 0:64], T.cA[:], A.add)
+    fill("l1", T.rst8[:, 0:64:8], 0.0)
+    ts("l1", T.hi[:], T.pi8[:], 0.125, None, A.mult)
+    ts("l1", T.lo[:], T.pi8[:], -0.125, 1.0, A.mult, A.add)
+    wait(V, "l1")
+    ts("l2", T.ci[:], T.nn[:], 3, None, A.arith_shift_right)
+    ts("l2", T.ti[:], T.ai[:], 3, None, A.arith_shift_right)
+    wait(V, "l2")
+    cp("l3", T.c8p[:, 1:65], T.ci[:])
+    wait(V, "l3")
+    scan("l4", T.nB[:], T.c8p[:, 0:64], T.rst8[:], 0.0, A.add, A.mult)
+    wait(V, "l4")
+    tt("l5", T.nBs[:], T.nB[:], T.cS[:], A.add)
+    tt("l5", T.tq[:], T.ti[:], T.nB[:], A.add)
+    wait(V, "l5")
+    for kk in range(4):
+        ts("l6", T.ge[:, 64 * kk:64 * kk + 64], T.nBs[:], T.nk[:, kk:kk + 1], BIG, A.is_ge, A.mult)
+    wait(V, "l6")
+    for kk in range(4):
+        scan("l7", T.sc[:, 64 * kk:64 * kk + 64], T.ge[:, 64 * kk:64 * kk + 64], T.tq[:], 0.0, A.max, A.min)
+    wait(V, "l7")
+    top = float(7 * SW + Q1)
+
+    def got(kk, y):
+        return T.sc[:, 64 * kk + 8 * pair2(me, 0)[y] + 7:64 * kk + 64:16]
+    ts("l8", T.ma[:], got(3, 0), T.kp8[:, 3:4], T.lo[:], A.add, A.mult)
+    ts("l8", T.mb[:], got(0, 1), T.kp8[:, 0:1], T.hi[:], A.add, A.mult)
+    for c in range(3):
+        ts("off2", T.off2[:, c:32:8], got(c, 0), T.kp8[:, c:c + 1], top, A.add, A.min)
+        ts("off2", T.off2[:, 4 + c:32:8], got(c + 1, 1), T.kp8[:, c + 1:c + 2], top, A.add, A.min)
+    wait(V, "l8")
+    tt("l9", T.mc[:], T.ma[:], T.mb[:], A.add)
+    ts("t8", T.t8[:], T.nB[:, 8 * me:8 * me + 8], -8.0, float(513 * 192 + 512 * (N - me)), A.mult, A.add)
+    wait(V, "l9")
+    ts("off2", T.off2[:, 3:32:8], T.mc[:], top, None, A.min)
+    wait(V, "t8")
+    for i in (0, 1, 16, 17):
+        tt("kin", T.kin[:, i:16 * (i // 16) + 16:2], T.t8[:], T.stf[:, 8 * me:8 * me + 8], A.subtract)
+    wait(V, "off2")
+    cp("ownm", T.ownm[:], T.off2[:, 8 * chip + 3:8 * chip + 7])
+    wait(V, "kin")
+    tr("kt", T.kt[:], T.kin[:])
+    wait(V, "w")
+    inc(V.quantize_mx(T.qw[:], T.sw[:], T.wt[:]), "qw")
+
+    wait(V, "own1c")
+    V.wait_ge(T.sem.p1c, n_in)
+    wait(S, "off2", "own1s")
+    S.wait_ge(T.sem.p1s, n_in)
+    for i, a, k in ((0, mine["split"], 7), (0, mine["carried"], 7), (1, mine["direct"], 7), (1, chip, 4)):
+        lst, cols = T.off2[:, 8 * a:8 * a + k], slice(2 * CAP * a, 2 * CAP * a + 16 * k)
+        cp("pk2c%d" % i, u32(T.slot2c[:, cols]), u32(T.land1c[:]).indirect(lst))
+        act("pk2s%d" % i, T.slot2s[:, cols], T.land1s[:].indirect(lst))
+    wait(V, "ownm")
+    cp("own2", u32(T.land2c[:, 0:SW]), u32(T.land1c[:]).indirect(T.ownm[:]))
+    wait(S, "ownm")
+    act("own2", T.land2s[:, 0:SW], T.land1s[:].indirect(T.ownm[:]))
+    v2, w2, r2 = view(T.slot2c, T.slot2s), view(T.land2c, T.land2s), view(T.rel2c, T.rel2s)
+
+    def at2(d):
+        return 2 * CAP * (d // 2) + CAP * pair2(me, d // 2).index(d)
+    send(2, lambda k, a: v2(k, slice(2 * CAP * a, 2 * CAP * a + 2 * CAP)), lambda k, d: v2(k, slice(at2(d), at2(d) + CAP)),
+         lambda k, d: w2(k, blk2(me, d)), lambda k: r2(k, slice(0, 2 * CAP)))
+
+    ts("d1", T.da[:], T.epar[:], 4.0, -2.0, A.mult, A.add)
+    ts("d1", T.db[:], T.epar[:], -1.0, 1.9375, A.mult, A.add)
+    ts("d1", T.j23[:], T.kp[:, 0:2], 23.0, None, A.min)
+    wait(V, "d1")
+    ts("d2", T.dl[:], T.pi1[:], T.da[:], T.db[:], A.mult, A.add)
+    wait(V, "d2")
+    ts("selD", T.selD[:], T.j23[:], T.dl[:], 16.0, A.add, A.mult)
+    wait(S, "X", "kt")
+    act("Xk", T.Xk[:], T.X[:], T.kt[:, 0:1], 513.0)
+    wait(V, "Xk")
+    tr("Xt", T.Xt[:], T.Xk[:])
+    wait(V, "Xt", "rstD")
+    scan("Xs", T.Xs[:], T.rstD[:], T.Xt[:], 0.0, A.add, A.max)
+    wait(V, "Xs", "selD")
+    cp("cd", T.cd[:], T.Xs[:].indirect(T.selD[:]))
+    wait(V, "cd")
+    ts("mk", T.mi[:], T.cd[:, 0:24], 9, 7, A.logical_shift_right, A.bitwise_and)
+    ts("mk", T.ki[:], T.cd[:, 0:24], 3, 63, A.logical_shift_right, A.bitwise_and)
+    wait(V, "mk")
+    ts("mf", T.mf[:], T.mi[:], float(CAP), 8.0, A.mult, A.add)
+    wait(V, "mf")
+    tt("sf", T.sf[:], T.mf[:], T.ki[:], A.add)
+    wait(V, "sf")
+    cp("off5", T.off5[:], T.sf[:])
+
+    h2 = L2 // 2
+    wait(TE, "qw", "own2")
+    TE.wait_ge(T.sem.p2c, n_in)
+    TE.wait_ge(T.sem.p2s, n_in)
+    for h in range(2):
+        cols = slice(h2 * h, h2 * h + h2)
+        inc(TE.matmul_mx(T.ps[:, 512 * h:512 * h + h2], T.qw[:], T.sw[:], T.land2c[:, cols], T.land2s[:, cols], True, True),
+            "mm%d" % h)
+    wait(S, "mm0")
+    act("ysb", T.ysb[:, 0:h2], T.ps[:, 0:h2])
+    wait(V, "mm1")
+    cp("ysb", T.ysb[:, h2:L2], T.ps[:, 512:512 + h2])
+    wait(V, "off5", "ysb")
+    wait(S, "off5", "ysb")
+    cp("yv", T.yo[:, 0:192], T.ysb[:].indirect(T.off5[:, 0:12]))
+    act("ys", T.yo[:, 192:T0], T.ysb[:].indirect(T.off5[:, 12:24]))
+    wait(Y, "yv")
+    dma(Y, "y", T.y[:, 0:192], T.yo[:, 0:192])
+    wait(S, "ys")
+    dma(S, "y", T.y[:, 192:T0], T.yo[:, 192:T0])
+    wait(Y, "y")
+    assert seen == count
+    g.wait_ge(T.sem.loc, ln[0])

@@ -6,6 +6,7 @@ R1 = Q1 + 1
 HALF = 4 * Q1 + 16
 L2 = 8 + N * CAP
 EMPTY = -1024
+NG = 6
 BIG = 65536.0
 ROUND = 12582912
 X4, U8, U16, F32, BF, I32 = "float8_e4m3fn_x4", "uint8", "uint16", "float32", "bfloat16", "int32"
@@ -18,25 +19,25 @@ def sb(n, t):
 SCRATCH = {
     "xt": sb(1536, BF), "wt": sb(512, BF), "qx": sb(T0, X4), "sx": sb(T0, U8), "qw": sb(128, X4), "sw": sb(128, U8),
     "slot1c": sb(2 * HALF, X4), "slot1s": sb(2 * HALF, U8), "land1c": sb(512, X4), "land1s": sb(512, U8),
-    "slot2c": sb(N * CAP, X4), "slot2s": sb(N * CAP, U8), "land2c": sb(L2, X4), "land2s": sb(L2, U8),
-    "relst": sb(8, U16), "rel1c": sb(Q1 + R1, X4), "rel1s": sb(Q1 + R1, U8), "rel2c": sb(2 * CAP, X4),
-    "rel2s": sb(2 * CAP, U8),
+    "slot2c": sb(N * SW, X4), "slot2s": sb(N * SW, U8), "land2c": sb(L2, X4), "land2s": sb(L2, U8),
+    "relst": sb(8, BF), "rel1c": sb(Q1 + R1, X4), "rel1s": sb(Q1 + R1, U8), "rel2c": sb(SW + CAP, X4),
+    "rel2s": sb(SW + CAP, U8),
     "tab": sb(12, I32), "tabk": sb(12, F32), "Lt": sb(108, F32), "C": sb(408, F32), "TT": sb(97, F32), "Sq": sb(64, F32),
     "F": sb(32, F32), "bc": sb(32, F32), "bct": sb(32, F32), "gd": sb(96, F32), "td": sb(96, F32), "pos": sb(96, F32),
     "e0": sb(36, F32), "e1": sb(36, F32), "e2": sb(36, F32), "off1": sb(12, U16), "torc": sb(192, BF),
     "win1": sb(416, BF), "trA": sb(416, BF), "trB": sb(T0, BF), "U": sb(32, F32), "sel": sb(2, U16), "g1": sb(32, U16),
-    "ownl": sb(4, U16), "pidx": sb(4, I32), "pi15": sb(4, I32), "pi16": sb(1, I32), "pi1": sb(1, I32), "pi8": sb(1, I32),
-    "par8": sb(1, F32), "epar": sb(1, F32), "k16": sb(4, F32), "kp": sb(4, F32), "kp8": sb(4, F32), "nk": sb(4, F32),
-    "lo": sb(1, F32), "hi": sb(1, F32), "j23": sb(2, F32), "da": sb(1, F32), "db": sb(1, F32), "dl": sb(1, F32),
-    "selD": sb(2, U16), "stage": sb(26, I32), "offp": sb(12, U16), "pb": sb(192, BF), "prow": sb(192, BF),
-    "e48": sb(48, BF), "win2": sb(N * T0, BF), "X": sb(416, BF), "Xk": sb(416, F32), "Xt": sb(416, F32),
-    "rstD": sb(416, F32), "Xs": sb(416, F32), "t8": sb(8, F32), "kin": sb(32, F32), "kt": sb(32, F32),
-    "cd": sb(32, I32), "mi": sb(24, I32), "ki": sb(24, I32), "mf": sb(24, F32), "sf": sb(24, F32), "off5": sb(24, U16),
-    "cA": sb(64, F32), "cS": sb(64, F32), "st": sb(64, U16), "stf": sb(72, F32), "nn": sb(64, I32), "ai": sb(64, I32),
-    "ci": sb(64, I32), "ti": sb(64, I32), "c8p": sb(66, F32), "rst8": sb(64, F32), "nB": sb(64, F32), "nBs": sb(64, F32),
-    "ge": sb(256, F32), "tq": sb(64, F32), "sc": sb(256, F32), "ma": sb(4, F32), "mb": sb(4, F32), "mc": sb(4, F32),
-    "off2": sb(32, U16), "ownm": sb(4, U16), "ysb": sb(L2, F32), "yo": sb(T0, F32),
-    "pd": ("dram", [8, 128, 6], BF), "lq": ("dram", [8, 128, 6], BF), "ps": ("psum", [128, 1024], F32),
+    "ownl": sb(4, U16), "pidx": sb(4, I32), "pi15": sb(4, I32), "pi16": sb(1, I32), "pi1": sb(1, I32),
+    "par8": sb(1, F32), "epar": sb(1, F32), "k16": sb(4, F32), "kp": sb(4, F32), "kpb": sb(4, F32),
+    "j23": sb(2, F32), "da": sb(1, F32), "db": sb(1, F32), "dl": sb(1, F32),
+    "selD": sb(2, U16), "stage": sb(33, I32), "offp": sb(4, U16), "pb": sb(64, BF), "prow": sb(64, BF),
+    "e48": sb(192, BF), "win2": sb(N * T0, BF), "X": sb(224, BF), "Xk": sb(224, F32), "Xt": sb(224, F32),
+    "rstD": sb(112, F32), "Xs": sb(224, F32), "t8": sb(8, F32), "kin": sb(32, F32), "kt": sb(32, F32),
+    "cd": sb(32, I32), "mi": sb(24, I32), "jw": sb(2, F32), "jx": sb(2, F32), "off5": sb(24, U16),
+    "cA": sb(64, F32), "st": sb(64, BF), "stf": sb(72, F32), "nn": sb(64, I32), "ai": sb(64, I32),
+    "ci": sb(64, I32), "ti": sb(64, I32), "c8p": sb(66, F32), "rst8": sb(64, F32), "nB": sb(64, F32),
+    "ge": sb(256, F32), "tq": sb(64, F32), "sc": sb(256, F32), "off2": sb(32, U16), "ysb": sb(N * SW, F32), "yo": sb(T0, F32),
+    "pd": ("dram", [N * NG, 128, 3], BF), "lq": ("dram", [N, 128, 3], BF), "rell": ("dram", [128, 3], BF),
+    "ps": ("psum", [128, 1024], F32),
 }
 SEMAPHORES = ["sst", "sls", "p1c", "p1s", "p2c", "p2s", "loc"] + ["s%d" % i for i in range(100)]
 
@@ -78,10 +79,6 @@ def u32(ap):
     return ap.bitcast(dt.uint32)
 
 
-def pair2(s, a):
-    return 2 * a + 1 - s % 2, 2 * a + s % 2
-
-
 def blk2(s, d):
     b = 8 + CAP * ((s - d) % N)
     return slice(b, b + CAP)
@@ -95,12 +92,12 @@ def hand_on(g, core, T, topo, ranks, plans):
         a = p["split"] if core == p["hf"] else p["carried"]
         ms = halves(topo.engines(core, ranks[2 * a]))
         l1, mst = slice(SW * s, SW * s + R1), T.st[:, 8 * s:8 * s + 8]
-        one, two = (2 * a, 2 * a + 1), pair2(s, a)
+        one = (2 * a, 2 * a + 1)
         steps = {
             "p1c": [(d, ms[y], u8(T.rel1c[:, Q1 * y:Q1 * y + R1]), u8(T.land1c[:, l1])) for y, d in enumerate(one)],
             "p1s": [(d, ms[y], T.rel1s[:, Q1 * y:Q1 * y + R1], T.land1s[:, l1]) for y, d in enumerate(one)],
-            "p2c": [(d, ms[y], u8(T.rel2c[:, CAP * y:CAP * y + CAP]), u8(T.land2c[:, blk2(s, d)])) for y, d in enumerate(two)],
-            "p2s": [(d, ms[y], T.rel2s[:, CAP * y:CAP * y + CAP], T.land2s[:, blk2(s, d)]) for y, d in enumerate(two)]}
+            "p2c": [(d, ms[y], u8(T.rel2c[:, SW * y:SW * y + CAP]), u8(T.land2c[:, blk2(s, d)])) for y, d in enumerate(one)],
+            "p2s": [(d, ms[y], T.rel2s[:, SW * y:SW * y + CAP], T.land2s[:, blk2(s, d)]) for y, d in enumerate(one)]}
         if core == p["hf"]:
             steps["sst"] = [(d, ms[y], T.relst[:], mst) for y, d in enumerate(one)]
             order, m_in = ["sst", "p1c", "p1s", "p2c", "p2s"], len(p["out"])
@@ -108,11 +105,14 @@ def hand_on(g, core, T, topo, ranks, plans):
             y = 0 if core == p["hc"] else 1
             steps["sst"] = [(one[y], ms[0] | ms[1], T.relst[:], mst)]
             order, m_in = ["sst", "p1" + "cs"[y], "p2" + "cs"[y]], len(p["home"])
+            if y == 0:
+                steps["sls"] = [(s, 1 << p["out"][0], T.rell[:], T.lq[s])]
+                order.insert(2, "sls")
         for sem in order:
-            g.wait_ge(T.sem[sem], m_in)
+            g.wait_ge(T.sem[sem], 1 if sem == "sls" else m_in)
             g.remote_dma_fused([RemoteDMATransfer(dst_ids=[dst_of(topo, ranks[d])], dma_engine_mask=m, remote_sem=T.sem[sem],
                                                   src=src, dst=dst) for d, m, src, dst in steps[sem]], local_sem=T.sem.loc)
-        g.wait_ge(T.sem.loc, len(order) * bits(ms[0] | ms[1]))
+        g.wait_ge(T.sem.loc, sum(bits(t[1]) for sem in order for t in steps[sem]))
 
 
 def rank_program(g, core, T, topo):
@@ -185,15 +185,14 @@ def rank_program(g, core, T, topo):
     iota("e", T.e0[:, 1:36:3], [[0, 12]], 1)
     iota("e", T.e0[:, 2:36:3], [[0, 12]], 1 - T0)
     iota("e", T.e1[:, 1:36:3], [[0, 12]], -ROUND)
-    iota("e48", T.e48[:], [[0, 48]], EMPTY)
-    iota("stage0", T.stage[:], [[1, 26]], 0, 24)
+    iota("stage0", T.stage[:], [[1, 33]], 0, 24)
+    iota("e48", T.e48[:], [[0, 192]], EMPTY)
     wait(Y, "stage0")
-    for h in range(2):
+    for q in range(NG):
+        u = 4 * (q // 2) + q % 2
         for e in range(2):
-            dma(Y, "stage", T.stage[16 * h:16 * h + 16, 1 - h + 12 * e:13 - h + 12 * e], T.to[8 * e:8 * e + 8, :])
-    iota("cA", T.cA[:], [[0, 4], [64 - 128 * par, 2], [8 * SW, 8]], 7 - me + 64 * par)
-    iota("cA", T.cS[:], [[0, 4], [8 - 16 * par, 2], [0, 8]], 8 * par - 8)
-    iota("pb0", T.pb[:], [[0, 192]], 0)
+            dma(Y, "stage", T.stage[16 * q:16 * q + 16, 9 - u + 12 * e:21 - u + 12 * e], T.to[8 * e:8 * e + 8, :])
+    iota("pb0", T.pb[:], [[0, 64]], 0)
     fill("k0", T.C[:, 11:408:12], 0.0)
     fill("k0", T.Lt[:, 0:12], 0.0)
     fill("k0", T.Lt[:, 96:108], 1.0)
@@ -210,9 +209,10 @@ def rank_program(g, core, T, topo):
     ts("sel", T.sel[:], T.kp[:, 0:2], 23.0, T.epar[:], A.min, A.add)
     wait(S, "par8", "torc0")
     act("torc", T.torc[:], T.torc[:], T.par8[:])
+    wait(S, "k2")
+    act("kpb", T.kpb[:], T.kp[:], 512.0, 1024.0)
     wait(Y, "e48")
-    for h in range(2):
-        dma(Y, "win2", T.win2[16 * h:16 * h + 1, :], T.e48[64 * h:64 * h + 64, :])
+    dma(Y, "win2", T.win2[0:16 * NG:16, :], T.e48[0:16 * NG, :])
     dma(Y, "w", T.wt[:], T.w[:])
 
     wait(V, "tab")
@@ -231,28 +231,41 @@ def rank_program(g, core, T, topo):
     scan("Sq", T.Sq[:], T.TT[:, 32:96], T.TT[:, 0:64], -4.5, A.add, A.subtract)
     wait(V, "Sq")
     tr("F", T.F[:], T.Sq[:, 32:64])
-    ts("bc", T.bc[:], T.Sq[:, 0:32], 0.0, T.Sq[:, 31:32], A.mult, A.add)
+    wait(S, "Sq")
+    act("bc", T.bc[:], T.Sq[:, 0:32], T.Sq[:, 31:32], 0.0)
     wait(V, "F")
     wait(S, "F")
-    for d in range(5):
-        ts("td", T.td[:, d:96:8], T.C[:, 12 + 12 * d:24 + 12 * d], T.F[:, d:d + 1], None, A.add)
-    for d in range(5, N):
-        act("td", T.td[:, d:96:8], T.C[:, 12 + 12 * d:24 + 12 * d], T.F[:, d:d + 1])
-    wait(V, "bc")
-    tr("bct", T.bct[:], T.bc[:])
+    for d in range(N):
+        if d == 1:
+            wait(V, "bc")
+            tr("bct", T.bct[:], T.bc[:])
+        if d < 5:
+            ts("td", T.td[:, d:96:8], T.C[:, 12 + 12 * d:24 + 12 * d], T.F[:, d:d + 1], None, A.add)
+        else:
+            act("td", T.td[:, d:96:8], T.C[:, 12 + 12 * d:24 + 12 * d], T.F[:, d:d + 1])
     wait(V, "td", "gd")
     scan("pos", T.pos[:], T.gd[:], T.td[:], 0.0, A.max, A.min)
-    wait(V, "bct")
     mst = T.st[:, 8 * me:8 * me + 8]
-    ts("sto", mst, T.bct[:, 0:8], 4.5, None, A.add)
+    wait(S, "bct")
+    act("sto", mst, T.bct[:, 0:8], 4.5 - 192.0)
     pos = T.pos[:, 7:96:8]
+    wait(S, "pos", "pb0")
+    for b in range(3):
+        act("pb", T.pb[32 * b:32 * b + 32, 0:64:16], T.pos[32 * b:32 * b + 32, 7 + 32 * b:32 + 32 * b:8], -188.5)
     wait(V, "pos")
     ts("qa", T.e1[:, 0:36:3], pos, 0.125, float(ROUND), A.mult, A.add)
     ts("qa", T.e1[:, 2:36:3], pos, 48.0, 184.0, A.mult, A.add)
     wait(V, "qa", "e")
     scan("e2", T.e2[:], T.e0[:], T.e1[:], 0.0, A.mult, A.add)
+    wait(V, "stage")
+    for e in range(2):
+        cp("prow", T.offp[:, e:4:2], T.stage[:, 9 + 12 * e:13 + 12 * e:2])
     wait(V, "e2")
     cp("off1", T.off1[:], T.e2[:, 2:36:3])
+    wait(V, "pb")
+    tr("prow", T.prow[:], T.pb[:])
+    wait(V, "prow", "win2")
+    cp("places", T.win2[:].indirect(T.offp[:]), T.prow[:])
     wait(V, "off1", "torc")
     cp("win1", T.win1[:].indirect(T.off1[:]), T.torc[:])
     wait(V, "x")
@@ -274,18 +287,18 @@ def rank_program(g, core, T, topo):
         cp("pk1c%d" % i, u32(T.slot1c[:, cols]), u32(T.qx[:]).indirect(lst))
         act("pk1s%d" % i, T.slot1s[:, cols], T.sx[:].indirect(lst))
     cp("ownl", T.ownl[:], T.g1[:, 3 * me:3 * me + 4])
-    wait(V, "pb0")
-    ts("pb", T.pb[:, 0:192:16], pos, -188.5, None, A.add)
     wait(V, "ownl")
     cp("own1c", u32(T.land1c[:, own1]), u32(T.qx[:]).indirect(T.ownl[:]))
     wait(S, "ownl")
     act("own1s", T.land1s[:, own1], T.sx[:].indirect(T.ownl[:]))
 
-    def send(ph, pair, single, land, rel):
+    def send(ph, pair, single, land, rel, between=None):
         for k in "cs":
             wait(g, "pk%d%s0" % (ph, k))
             fused([(out, "p%d%s" % (ph, k), pair(k, mine["split"]), [(mine["hf"], rel(k))]),
                    (home, "p%d%s" % (ph, k), pair(k, mine["carried"]), [(mine["h" + k], rel(k))])])
+        if between:
+            between()
         for k in "cs":
             wait(g, "pk%d%s1" % (ph, k))
             fused([(outs[y], "p%d%s" % (ph, k), single(k, d), [(ranks[d], land(k, d))])
@@ -297,152 +310,136 @@ def rank_program(g, core, T, topo):
     wait(g, "sto")
     fused([(out, "sst", mst, [(mine["hf"], T.relst[:])] + [(ranks[2 * mine["direct"] + y], mst) for y in range(2)]),
            (home, "sst", mst, [(mine["hc"], T.relst[:]), (mine["hs"], T.relst[:]), (ranks[mine["near"]], mst)])])
+    iota("cA", T.cA[:], [[0, 8], [8 * SW, 8]], 7 - me)
+    iota("cA", T.stf[:, 64:72], [[0, 8]], T0)
+    iota("cA", T.rst8[:], [[0, 64]], 1)
+    iota("rst8", T.c8p[:, 0:1], [[0, 1]], 0)
+    wait(g, "cA")
+    iota("rst8", T.rst8[:, 0:64:8], [[0, 8]], 0)
+    iota("X0", T.X[:], [[0, 224]], EMPTY)
+    wait(Y, "places")
+    dma(Y, "pd", T.pd[:], T.win2[0:16 * NG:16, :])
+
+    def tables():
+        wait(g, "pd")
+        far = [d for d in range(N) if d // 2 != chip]
+        ways = ([(mine["out"][i], d, ranks[d], T.lq[me]) for i, d in enumerate(far)]
+                + [(mine["home"][0], mine["near"], ranks[mine["near"]], T.lq[me]), (mine["home"][1], me, mine["hc"], T.rell[:])])
+        g.remote_dma_fused([RemoteDMATransfer(dst_ids=[dst_of(topo, c)], dma_engine_mask=1 << e, remote_sem=T.sem.sls, alu_op=2,
+                                              srcs=[T.pd[N * q + d] for q in range(NG)], dsts=[to]) for e, d, c, to in ways],
+                           local_sem=T.sem.loc)
+        ln[0] += N
     v1, w1, r1 = view(T.slot1c, T.slot1s), view(T.land1c, T.land1s), view(T.rel1c, T.rel1s)
 
     def at1(d):
         return HALF * (d // 4) + Q1 * (d % 4)
     send(1, lambda k, a: v1(k, slice(at1(2 * a), at1(2 * a) + Q1 + R1)), lambda k, d: v1(k, slice(at1(d), at1(d) + R1)),
-         lambda k, d: w1(k, slice(SW * me, SW * me + R1)), lambda k: r1(k, slice(0, Q1 + R1)))
-    iota("X0", T.X[:], [[0, 416]], EMPTY)
-    iota("rst0", T.rstD[:], [[0, 416]], 0)
+         lambda k, d: w1(k, slice(SW * me, SW * me + R1)), lambda k: r1(k, slice(0, Q1 + R1)), tables)
+    iota("rst0", T.rstD[:], [[0, 112]], 0)
     wait(g, "rst0")
-    iota("rstD", T.rstD[:, 0:416:16], [[0, 26]], -ROUND)
-
-    wait(V, "pb")
-    tr("prow", T.prow[:], T.pb[:])
-    wait(V, "stage")
-    for e in range(2):
-        cp("offp", T.offp[:, e:12:2], T.stage[:, 12 * e + 1:12 * e + 13:2])
-    wait(V, "prow", "offp", "win2")
-    cp("places", T.win2[:].indirect(T.offp[:]), T.prow[:])
-    wait(Y, "places")
-    for h in range(2):
-        dma(Y, "pd", T.pd[:, 64 * h:64 * h + 64, :], T.win2[16 * h:16 * h + 1, :])
-    for h in range(2):
-        dma(Y, "lq", T.lq[me, 64 * h:64 * h + 64, :], T.win2[16 * h:16 * h + 1, T0 * me:T0 * me + T0])
-    wait(g, "pd")
-    far = [d for d in range(N) if d // 2 != chip]
-    fused([(1 << mine["out"][i], "sls", T.pd[d], [(ranks[d], T.lq[me])]) for i, d in enumerate(far)]
-          + [(1 << mine["home"][0], "sls", T.pd[mine["near"]], [(ranks[mine["near"]], T.lq[me])])])
-    Y.wait_ge(T.sem.sls, N - 1)
-    wait(Y, "lq", "X0")
+    iota("rstD", T.rstD[:, 0:112:8], [[0, 14]], -ROUND)
+    Y.wait_ge(T.sem.sls, N)
+    wait(Y, "X0")
     for q in range(8):
-        dma(Y, "X", T.X[16 * q:16 * q + 16, 16 * (q % 2):16 * (q % 2) + T0], T.lq[:])
+        dma(Y, "X", T.X[16 * q:16 * q + 16, 16 * (q % 2):16 * (q % 2) + 192], T.lq[:])
 
-    fill("k3", T.stf[:, 64:72], float(T0))
-    fill("k3", T.c8p[:, 0:1], 0.0)
-    fill("k3", T.rst8[:], 1.0)
-    ts("k3", T.pi8[:], T.pidx[:, 0:1], 8, None, A.bitwise_and)
-    ts("k3", T.pi1[:], T.pidx[:, 0:1], 1, None, A.bitwise_and)
-    ts("k3", T.kp8[:], T.kp[:], -8.0, None, A.add)
-    ts("k3", T.nk[:], T.kp[:], -1.0, None, A.mult)
-    V.wait_ge(T.sem.sst, n_st)
+    for q in (V, S):
+        q.wait_ge(T.sem.sst, n_st)
     wait(V, "sto")
     for d in range(N):
-        cp("k3", T.stf[:, 8 * d:8 * d + 8], T.st[:, d:64:8])
-    wait(V, "k3", "cA")
+        if d < 5:
+            ts("stf", T.stf[:, 8 * d:8 * d + 8], T.st[:, d:64:8], 192.0, None, A.add)
+        else:
+            act("stf", T.stf[:, 8 * d:8 * d + 8], T.st[:, d:64:8], 192.0)
+    wait(V, "stf", "cA")
     tt("l1", T.nn[:], T.stf[:, 0:64], T.stf[:, 8:72], A.subtract)
     tt("l1", T.ai[:], T.stf[:, 0:64], T.cA[:], A.add)
-    fill("l1", T.rst8[:, 0:64:8], 0.0)
-    ts("l1", T.hi[:], T.pi8[:], 0.125, None, A.mult)
-    ts("l1", T.lo[:], T.pi8[:], -0.125, 1.0, A.mult, A.add)
     wait(V, "l1")
     ts("l2", T.ci[:], T.nn[:], 3, None, A.arith_shift_right)
-    ts("l2", T.ti[:], T.ai[:], 3, None, A.arith_shift_right)
+    ts("l3", T.ti[:], T.ai[:], 3, None, A.arith_shift_right)
     wait(V, "l2")
     cp("l3", T.c8p[:, 1:65], T.ci[:])
-    wait(V, "l3")
-    scan("l4", T.nB[:], T.c8p[:, 0:64], T.rst8[:], 0.0, A.add, A.mult)
-    wait(V, "l4")
-    tt("l5", T.nBs[:], T.nB[:], T.cS[:], A.add)
-    tt("l5", T.tq[:], T.ti[:], T.nB[:], A.add)
-    wait(V, "l5")
+    wait(V, "l3", "rst8")
+    scan("nB", T.nB[:], T.c8p[:, 0:64], T.rst8[:], 0.0, A.add, A.mult)
+    wait(V, "nB", "kpb")
+    wait(S, "nB")
+    tt("ge0", T.tq[:], T.ti[:], T.nB[:], A.add)
     for kk in range(4):
-        ts("l6", T.ge[:, 64 * kk:64 * kk + 64], T.nBs[:], T.nk[:, kk:kk + 1], BIG, A.is_ge, A.mult)
-    wait(V, "l6")
+        ge = T.ge[:, 64 * kk:64 * kk + 64]
+        if kk < 2:
+            ts("ge0", ge, T.nB[:], 1024.0, T.kpb[:, kk:kk + 1], A.mult, A.add)
+        else:
+            act("ge2", ge, T.nB[:], T.kpb[:, kk:kk + 1], 1024.0)
     for kk in range(4):
+        if kk % 2 == 0:
+            wait(V, "ge%d" % kk)
         scan("l7", T.sc[:, 64 * kk:64 * kk + 64], T.ge[:, 64 * kk:64 * kk + 64], T.tq[:], 0.0, A.max, A.min)
     wait(V, "l7")
-    top = float(7 * SW + Q1)
+    for kk in range(4):
+        ts("off2", T.off2[:, kk:32:4], T.sc[:, 64 * kk + 7:64 * kk + 64:8], T.kp[:, kk:kk + 1], float(7 * SW + Q1), A.add, A.min)
 
-    def got(kk, y):
-        return T.sc[:, 64 * kk + 8 * pair2(me, 0)[y] + 7:64 * kk + 64:16]
-    ts("l8", T.ma[:], got(3, 0), T.kp8[:, 3:4], T.lo[:], A.add, A.mult)
-    ts("l8", T.mb[:], got(0, 1), T.kp8[:, 0:1], T.hi[:], A.add, A.mult)
-    for c in range(3):
-        ts("off2", T.off2[:, c:32:8], got(c, 0), T.kp8[:, c:c + 1], top, A.add, A.min)
-        ts("off2", T.off2[:, 4 + c:32:8], got(c + 1, 1), T.kp8[:, c + 1:c + 2], top, A.add, A.min)
-    wait(V, "l8")
-    tt("l9", T.mc[:], T.ma[:], T.mb[:], A.add)
-    ts("t8", T.t8[:], T.nB[:, 8 * me:8 * me + 8], -8.0, float(513 * 192 + 512 * (N - me)), A.mult, A.add)
-    wait(V, "l9")
-    ts("off2", T.off2[:, 3:32:8], T.mc[:], top, None, A.min)
-    wait(V, "t8")
-    for i in (0, 1, 16, 17):
-        tt("kin", T.kin[:, i:16 * (i // 16) + 16:2], T.t8[:], T.stf[:, 8 * me:8 * me + 8], A.subtract)
-    wait(V, "off2")
-    cp("ownm", T.ownm[:], T.off2[:, 8 * chip + 3:8 * chip + 7])
-    wait(V, "kin")
-    tr("kt", T.kt[:], T.kin[:])
-    wait(V, "w")
-    inc(V.quantize_mx(T.qw[:], T.sw[:], T.wt[:]), "qw")
-
-    wait(V, "own1c")
+    wait(V, "own1c", "off2")
     V.wait_ge(T.sem.p1c, n_in)
     wait(S, "off2", "own1s")
     S.wait_ge(T.sem.p1s, n_in)
-    for i, a, k in ((0, mine["split"], 7), (0, mine["carried"], 7), (1, mine["direct"], 7), (1, chip, 4)):
-        lst, cols = T.off2[:, 8 * a:8 * a + k], slice(2 * CAP * a, 2 * CAP * a + 16 * k)
+    three = sorted((2 * mine["direct"], 2 * mine["direct"] + 1, mine["near"]))
+    runs = [(0, 4 * (mine["split"] // 2), 4)]
+    runs += [(1, three[0], 3)] if three[2] - three[0] == 2 else [(1, 2 * mine["direct"], 2), (1, mine["near"], 1)]
+    for i, d, k in runs:
+        lst, cols = T.off2[:, 4 * d:4 * (d + k)], slice(SW * d, SW * (d + k))
         cp("pk2c%d" % i, u32(T.slot2c[:, cols]), u32(T.land1c[:]).indirect(lst))
         act("pk2s%d" % i, T.slot2s[:, cols], T.land1s[:].indirect(lst))
-    wait(V, "ownm")
-    cp("own2", u32(T.land2c[:, 0:SW]), u32(T.land1c[:]).indirect(T.ownm[:]))
-    wait(S, "ownm")
-    act("own2", T.land2s[:, 0:SW], T.land1s[:].indirect(T.ownm[:]))
+    cp("own2", u32(T.land2c[:, 0:SW]), u32(T.land1c[:]).indirect(T.off2[:, 4 * me:4 * me + 4]))
+    act("own2", T.land2s[:, 0:SW], T.land1s[:].indirect(T.off2[:, 4 * me:4 * me + 4]))
     v2, w2, r2 = view(T.slot2c, T.slot2s), view(T.land2c, T.land2s), view(T.rel2c, T.rel2s)
+    send(2, lambda k, a: v2(k, slice(2 * SW * a, 2 * SW * a + SW + CAP)), lambda k, d: v2(k, slice(SW * d, SW * d + CAP)),
+         lambda k, d: w2(k, blk2(me, d)), lambda k: r2(k, slice(0, SW + CAP)))
 
-    def at2(d):
-        return 2 * CAP * (d // 2) + CAP * pair2(me, d // 2).index(d)
-    send(2, lambda k, a: v2(k, slice(2 * CAP * a, 2 * CAP * a + 2 * CAP)), lambda k, d: v2(k, slice(at2(d), at2(d) + CAP)),
-         lambda k, d: w2(k, blk2(me, d)), lambda k: r2(k, slice(0, 2 * CAP)))
-
+    ts("t8", T.t8[:], T.nB[:, 8 * me:8 * me + 8], -8.0, float(513 * 192 + 512 * (N - me)), A.mult, A.add)
+    wait(V, "w")
+    inc(V.quantize_mx(T.qw[:], T.sw[:], T.wt[:]), "qw")
+    wait(V, "t8")
+    for i in (0, 1, 16, 17):
+        tt("kin", T.kin[:, i:16 * (i // 16) + 16:2], T.t8[:], T.stf[:, 8 * me:8 * me + 8], A.subtract)
+    wait(V, "kin")
+    tr("kt", T.kt[:], T.kin[:])
+    ts("d1", T.pi1[:], T.pidx[:, 0:1], 1, None, A.bitwise_and)
     ts("d1", T.da[:], T.epar[:], 4.0, -2.0, A.mult, A.add)
-    ts("d1", T.db[:], T.epar[:], -1.0, 1.9375, A.mult, A.add)
+    ts("d1", T.db[:], T.epar[:], -1.0, 1.875, A.mult, A.add)
     ts("d1", T.j23[:], T.kp[:, 0:2], 23.0, None, A.min)
+    ts("d1", T.jw[:], T.kp[:, 0:2], 12.0, 2.0, A.is_ge, A.mult)
     wait(V, "d1")
     ts("d2", T.dl[:], T.pi1[:], T.da[:], T.db[:], A.mult, A.add)
+    tt("d2", T.jx[:], T.j23[:], T.jw[:], A.add)
     wait(V, "d2")
-    ts("selD", T.selD[:], T.j23[:], T.dl[:], 16.0, A.add, A.mult)
+    ts("selD", T.selD[:], T.jx[:], T.dl[:], 8.0, A.add, A.mult)
     wait(S, "X", "kt")
     act("Xk", T.Xk[:], T.X[:], T.kt[:, 0:1], 513.0)
     wait(V, "Xk")
     tr("Xt", T.Xt[:], T.Xk[:])
     wait(V, "Xt", "rstD")
-    scan("Xs", T.Xs[:], T.rstD[:], T.Xt[:], 0.0, A.add, A.max)
+    for w in range(2):
+        scan("Xs", T.Xs[:, 112 * w:112 * w + 112], T.rstD[:], T.Xt[:, w:224:2], 0.0, A.add, A.max)
     wait(V, "Xs", "selD")
     cp("cd", T.cd[:], T.Xs[:].indirect(T.selD[:]))
     wait(V, "cd")
-    ts("mk", T.mi[:], T.cd[:, 0:24], 9, 7, A.logical_shift_right, A.bitwise_and)
-    ts("mk", T.ki[:], T.cd[:, 0:24], 3, 63, A.logical_shift_right, A.bitwise_and)
+    ts("mk", T.mi[:], T.cd[:, 0:24], 3, N * SW - 1, A.logical_shift_right, A.bitwise_and)
     wait(V, "mk")
-    ts("mf", T.mf[:], T.mi[:], float(CAP), 8.0, A.mult, A.add)
-    wait(V, "mf")
-    tt("sf", T.sf[:], T.mf[:], T.ki[:], A.add)
-    wait(V, "sf")
-    cp("off5", T.off5[:], T.sf[:])
+    cp("off5", T.off5[:], T.mi[:])
 
-    h2 = L2 // 2
+    h2 = 8 + 4 * CAP
     wait(TE, "qw", "own2")
     TE.wait_ge(T.sem.p2c, n_in)
     TE.wait_ge(T.sem.p2s, n_in)
-    for h in range(2):
-        cols = slice(h2 * h, h2 * h + h2)
-        inc(TE.matmul_mx(T.ps[:, 512 * h:512 * h + h2], T.qw[:], T.sw[:], T.land2c[:, cols], T.land2s[:, cols], True, True),
+    for h, (a, b) in enumerate(((0, h2), (h2, L2))):
+        inc(TE.matmul_mx(T.ps[:, 512 * h:512 * h + b - a], T.qw[:], T.sw[:], T.land2c[:, a:b], T.land2s[:, a:b], True, True),
             "mm%d" % h)
     wait(S, "mm0")
-    act("ysb", T.ysb[:, 0:h2], T.ps[:, 0:h2])
     wait(V, "mm1")
-    cp("ysb", T.ysb[:, h2:L2], T.ps[:, 512:512 + h2])
+    for m in range(4):
+        a = 8 + CAP * m if m else 0
+        act("ysb", T.ysb[:, SW * m:SW * m + CAP], T.ps[:, a:a + CAP])
+        cp("ysb", T.ysb[:, SW * (m + 4):SW * (m + 4) + CAP], T.ps[:, 512 + CAP * m:512 + CAP * m + CAP])
     wait(V, "off5", "ysb")
     wait(S, "off5", "ysb")
     cp("yv", T.yo[:, 0:192], T.ysb[:].indirect(T.off5[:, 0:12]))

@@ -3,7 +3,7 @@ from concourse.mybir import dt, AluOpType as A, ActivationFunctionType as AF
 
 T0, N, Q1, CAP, SW = 384, 8, 48, 56, 64
 R1 = Q1 + 1
-HALF = 4 * Q1 + 16
+PAIR, HALF = 2 * Q1 + 16, 4 * Q1 + 16
 L2 = 8 + N * CAP
 EMPTY = -1024
 NG = 6
@@ -18,28 +18,29 @@ def sb(n, t):
 
 SCRATCH = {
     "xt": sb(1536, BF), "wt": sb(512, BF), "qx": sb(T0, X4), "sx": sb(T0, U8), "qw": sb(128, X4), "sw": sb(128, U8),
-    "slot1c": sb(2 * HALF, X4), "slot1s": sb(2 * HALF, U8), "land1c": sb(512, X4), "land1s": sb(512, U8),
+    "slot1c": sb(2 * PAIR + HALF, X4), "slot1s": sb(2 * PAIR + HALF, U8), "land1c": sb(512, X4), "land1s": sb(512, U8),
     "slot2c": sb(N * SW, X4), "slot2s": sb(N * SW, U8), "land2c": sb(L2, X4), "land2s": sb(L2, U8),
     "relst": sb(8, BF), "rel1c": sb(Q1 + R1, X4), "rel1s": sb(Q1 + R1, U8), "rel2c": sb(SW + CAP, X4),
     "rel2s": sb(SW + CAP, U8),
-    "tab": sb(12, I32), "tabk": sb(12, F32), "Lt": sb(108, F32), "C": sb(408, F32), "TT": sb(97, F32), "Sq": sb(64, F32),
-    "F": sb(32, F32), "bc": sb(32, F32), "bct": sb(32, F32), "gd": sb(96, F32), "td": sb(96, F32), "pos": sb(96, F32),
+    "tab": sb(16, I32), "Lt": sb(144, F32), "C": sb(544, F32), "thr": sb(128, F32), "l16": sb(8, U16),
+    "TT": sb(161, F32), "Sq": sb(64, F32),
+    "F": sb(32, F32), "bc": sb(64, BF), "bct": sb(32, BF), "gd": sb(96, F32), "td": sb(96, F32), "pos": sb(96, F32),
     "e0": sb(36, F32), "e1": sb(36, F32), "e2": sb(36, F32), "off1": sb(12, U16), "torc": sb(192, BF),
     "win1": sb(416, BF), "trA": sb(416, BF), "trB": sb(T0, BF), "U": sb(32, F32), "sel": sb(2, U16), "g1": sb(32, U16),
-    "ownl": sb(4, U16), "pidx": sb(4, I32), "pi15": sb(4, I32), "pi16": sb(1, I32), "pi1": sb(1, I32),
-    "par8": sb(1, F32), "epar": sb(1, F32), "k16": sb(4, F32), "kp": sb(4, F32), "kpb": sb(4, F32),
-    "j23": sb(2, F32), "da": sb(1, F32), "db": sb(1, F32), "dl": sb(1, F32),
+    "ownl": sb(4, U16), "pidx": sb(8, I32), "pi15": sb(8, I32), "pi16": sb(1, I32), "pi1": sb(1, I32),
+    "par8": sb(1, F32), "epar": sb(1, F32), "k16": sb(8, F32), "kp": sb(4, F32), "kpb": sb(4, F32),
+    "da": sb(1, F32), "db": sb(1, F32), "dl": sb(1, F32),
     "selD": sb(2, U16), "stage": sb(33, I32), "offp": sb(4, U16), "pb": sb(64, BF), "prow": sb(64, BF),
-    "e48": sb(192, BF), "win2": sb(N * T0, BF), "X": sb(224, BF), "Xk": sb(224, F32), "Xt": sb(224, F32),
+    "e48": sb(224, BF), "win2": sb(N * T0, BF), "X": sb(224, BF), "Xk": sb(224, F32), "Xt": sb(224, F32),
     "rstD": sb(112, F32), "Xs": sb(224, F32), "t8": sb(8, F32), "kin": sb(32, F32), "kt": sb(32, F32),
     "cd": sb(32, I32), "mi": sb(24, I32), "jw": sb(2, F32), "jx": sb(2, F32), "off5": sb(24, U16),
-    "cA": sb(64, F32), "st": sb(64, BF), "stf": sb(72, F32), "nn": sb(64, I32), "ai": sb(64, I32),
+    "cA": sb(64, F32), "st": sb(64, BF), "stf": sb(72, F32), "cB": sb(64, F32),
     "ci": sb(64, I32), "ti": sb(64, I32), "c8p": sb(66, F32), "rst8": sb(64, F32), "nB": sb(64, F32),
     "ge": sb(256, F32), "tq": sb(64, F32), "sc": sb(256, F32), "off2": sb(32, U16), "ysb": sb(N * SW, F32), "yo": sb(T0, F32),
-    "pd": ("dram", [N * NG, 128, 3], BF), "lq": ("dram", [N, 128, 3], BF), "rell": ("dram", [128, 3], BF),
-    "ps": ("psum", [128, 1024], F32),
+    "pd": ("dram", [N * NG, 128, 3], BF), "lq": ("dram", [N, 128, 3], BF), "rell": ("dram", [N, 128, 3], BF),
+    "ps": ("psum", [128, 2048], F32),
 }
-SEMAPHORES = ["sst", "sls", "p1c", "p1s", "p2c", "p2s", "loc"] + ["s%d" % i for i in range(100)]
+SEMAPHORES = ["sst", "sls", "p1c", "p1s", "p2c", "p2s", "loc"] + ["s%d" % i for i in range(120)]
 
 
 def bits(m):
@@ -90,26 +91,26 @@ def hand_on(g, core, T, topo, ranks, plans):
         if core not in (p["hc"], p["hs"], p["hf"]):
             continue
         a = p["split"] if core == p["hf"] else p["carried"]
-        ms = halves(topo.engines(core, ranks[2 * a]))
+        es = topo.engines(core, ranks[2 * a])
+        ms = halves(es)
         l1, mst = slice(SW * s, SW * s + R1), T.st[:, 8 * s:8 * s + 8]
-        one = (2 * a, 2 * a + 1)
+        two = (2 * a, 2 * a + 1)
         steps = {
-            "p1c": [(d, ms[y], u8(T.rel1c[:, Q1 * y:Q1 * y + R1]), u8(T.land1c[:, l1])) for y, d in enumerate(one)],
-            "p1s": [(d, ms[y], T.rel1s[:, Q1 * y:Q1 * y + R1], T.land1s[:, l1]) for y, d in enumerate(one)],
-            "p2c": [(d, ms[y], u8(T.rel2c[:, SW * y:SW * y + CAP]), u8(T.land2c[:, blk2(s, d)])) for y, d in enumerate(one)],
-            "p2s": [(d, ms[y], T.rel2s[:, SW * y:SW * y + CAP], T.land2s[:, blk2(s, d)]) for y, d in enumerate(one)]}
+            "p1c": [(d, ms[y], u8(T.rel1c[:, Q1 * y:Q1 * y + R1]), u8(T.land1c[:, l1])) for y, d in enumerate(two)],
+            "p1s": [(d, ms[y], T.rel1s[:, Q1 * y:Q1 * y + R1], T.land1s[:, l1]) for y, d in enumerate(two)],
+            "p2c": [(d, ms[y], u8(T.rel2c[:, SW * y:SW * y + CAP]), u8(T.land2c[:, blk2(s, d)])) for y, d in enumerate(two)],
+            "p2s": [(d, ms[y], T.rel2s[:, SW * y:SW * y + CAP], T.land2s[:, blk2(s, d)]) for y, d in enumerate(two)]}
+        m_in = len(p["home"])
         if core == p["hf"]:
-            steps["sst"] = [(d, ms[y], T.relst[:], mst) for y, d in enumerate(one)]
-            order, m_in = ["sst", "p1c", "p1s", "p2c", "p2s"], len(p["out"])
+            steps["sst"] = [(d, ms[y], T.relst[:], mst) for y, d in enumerate(two)]
+            order = ["sst", "p1c", "p1s", "p2c", "p2s"]
         else:
             y = 0 if core == p["hc"] else 1
-            steps["sst"] = [(one[y], ms[0] | ms[1], T.relst[:], mst)]
-            order, m_in = ["sst", "p1" + "cs"[y], "p2" + "cs"[y]], len(p["home"])
-            if y == 0:
-                steps["sls"] = [(s, 1 << p["out"][0], T.rell[:], T.lq[s])]
-                order.insert(2, "sls")
+            steps["sst"] = [(two[y], ms[0] | ms[1], T.relst[:], mst)]
+            steps["sls"] = [(d, 1 << es[d], T.rell[d], T.lq[s]) for d in range(N)]
+            order = ["sst", "p1c", "p2c"] if y == 0 else ["sst", "sls", "p1s", "p2s"]
         for sem in order:
-            g.wait_ge(T.sem[sem], 1 if sem == "sls" else m_in)
+            g.wait_ge(T.sem[sem], m_in // 2 if sem == "sst" and core != p["hf"] else m_in)
             g.remote_dma_fused([RemoteDMATransfer(dst_ids=[dst_of(topo, ranks[d])], dma_engine_mask=m, remote_sem=T.sem[sem],
                                                   src=src, dst=dst) for d, m, src, dst in steps[sem]], local_sem=T.sem.loc)
         g.wait_ge(T.sem.loc, sum(bits(t[1]) for sem in order for t in steps[sem]))
@@ -171,105 +172,139 @@ def rank_program(g, core, T, topo):
 
     out, home = mask_of(mine["out"]), mask_of(mine["home"])
     outs = halves(mine["out"])
-    n_in = 2 * bits(outs[0]) + bits(home) + (bits(out) + bits(home)) + 2 * bits(outs[0])
+    n_c = n_s = 2 * bits(outs[0]) + bits(home) + (bits(out) + bits(home)) + 2 * bits(outs[0])
     n_st = 2 * bits(out) + bits(home) + (bits(out) + bits(home)) + 2 * bits(out)
 
     for q in range(4):
-        dma(Y if q % 2 == 0 else S, "tab", T.tab[32 * q:32 * q + 32, :], T.to[:])
-    dma(S, "x", T.xt[:], T.x[:])
+        dma(Y if q % 2 == 0 else S, "tab", T.tab[32 * q:32 * q + 32, 0:12], T.to[:])
 
-    iota("pidx", T.pidx[:], [[0, 4]], 0, 1)
-    iota("pidx", T.k16[:], [[16, 4]], 0)
-    iota("torc0", T.torc[:], [[16, 12], [1, 8], [192, 2]], -192)
-    iota("e", T.e0[:, 0:36:3], [[0, 12]], 0)
-    iota("e", T.e0[:, 1:36:3], [[0, 12]], 1)
-    iota("e", T.e0[:, 2:36:3], [[0, 12]], 1 - T0)
-    iota("e", T.e1[:, 1:36:3], [[0, 12]], -ROUND)
+    def quantize(i):
+        wait(V, "x%d" % i)
+        inc(V.quantize_mx(T.qx[:, 128 * i:128 * i + 128], T.sx[:, 128 * i:128 * i + 128], T.xt[:, 512 * i:512 * i + 512]), "qx")
     iota("stage0", T.stage[:], [[1, 33]], 0, 24)
-    iota("e48", T.e48[:], [[0, 192]], EMPTY)
+    iota("pidx", T.pidx[:], [[0, 8]], 0, 1)
+    fill("e48", T.e48[:], float(EMPTY))
     wait(Y, "stage0")
-    for q in range(NG):
-        u = 4 * (q // 2) + q % 2
-        for e in range(2):
-            dma(Y, "stage", T.stage[16 * q:16 * q + 16, 9 - u + 12 * e:21 - u + 12 * e], T.to[8 * e:8 * e + 8, :])
-    iota("pb0", T.pb[:], [[0, 64]], 0)
-    fill("k0", T.C[:, 11:408:12], 0.0)
-    fill("k0", T.Lt[:, 0:12], 0.0)
-    fill("k0", T.Lt[:, 96:108], 1.0)
-    fill("k0", T.TT[:, 0:65], 0.0)
-    fill("k0", T.win1[:], 0.0)
+
+    def stage(queue, e):
+        for q in range(NG):
+            u = 4 * (q // 2) + q % 2
+            dma(queue, "stage", T.stage[16 * q:16 * q + 16, 9 - u + 12 * e:21 - u + 12 * e], T.to[8 * e:8 * e + 8, :])
+    stage(Y, 0)
+    wait(Y, "e48")
+    dma(Y, "win2", T.win2[0:16 * NG:16, :], T.e48[0:16 * NG, 0:192])
+
+    iota("thr", T.thr[:], [[T0, 8], [0, 16]], T0)
+    iota("k16", T.k16[:], [[16, 8]], 0)
+    iota("torc0", T.torc[:], [[16, 12], [1, 8], [192, 2]], -192)
+    iota("cA0", T.cA[:], [[-7, 8], [16 * SW, 8]], 7 - 2 * me)
+    fill("k0", T.tab[:, 12:16], N * T0)
+    fill("k0", T.Lt[:, 0:16], 0.0)
+    fill("k0", T.C[:, 15:544:16], 0.0)
     wait(V, "pidx")
     ts("k1", T.pi15[:], T.pidx[:], 15, None, A.bitwise_and)
     ts("k1", T.pi16[:], T.pidx[:, 0:1], 16, None, A.bitwise_and)
     wait(V, "k1")
-    ts("par8", T.par8[:], T.pi16[:], 0.5, None, A.mult)
+    cp("k0", T.l16[:], T.pi15[:])
     ts("k2", T.epar[:], T.pi16[:], -0.0625, 1.0, A.mult, A.add)
-    tt("k2", T.kp[:], T.pi15[:], T.k16[:], A.add)
+    dma(S, "x0", T.xt[:, 0:512], T.x[:, 0:512])
+    wait(S, "stage0")
+    stage(S, 1)
+    for i in (1, 2):
+        dma(S, "x%d" % i, T.xt[:, 512 * i:512 * i + 512], T.x[:, 512 * i:512 * i + 512])
+    wait(S, "e48")
+    act("z0", T.TT[:], T.e48[:, 0:161], 0.0, 0.0)
+
+    wait(V, "tab", "k0", "thr")
+    tt("Lt", T.Lt[:, 16:144], T.tab[:].indirect(T.l16[:]), T.thr[:], A.is_lt)
+    wait(V, "k16")
+    tt("k2", T.kp[:], T.pi15[:, 0:4], T.k16[:, 0:4], A.add)
+    wait(V, "Lt")
+    scan("C", T.C[:, 16:144], T.Lt[:, 16:144], T.Lt[:, 0:128], 0.0, A.add, A.subtract)
     wait(V, "k2")
     ts("sel", T.sel[:], T.kp[:, 0:2], 23.0, T.epar[:], A.min, A.add)
-    wait(S, "par8", "torc0")
-    act("torc", T.torc[:], T.torc[:], T.par8[:])
-    wait(S, "k2")
-    act("kpb", T.kpb[:], T.kp[:], 512.0, 1024.0)
-    wait(Y, "e48")
-    dma(Y, "win2", T.win2[0:16 * NG:16, :], T.e48[0:16 * NG, :])
-    dma(Y, "w", T.wt[:], T.w[:])
-
-    wait(V, "tab")
-    for d in range(1, N):
-        ts("Lt", T.Lt[:, 12 * d:12 * d + 12], T.tab[:], float(T0 * d), None, A.is_lt)
-    cp("tabk", T.tabk[:], T.tab[:])
-    wait(V, "k0", "Lt")
-    scan("C", T.C[:, 12:108], T.Lt[:, 12:108], T.Lt[:, 0:96], 0.0, A.add, A.subtract)
-    wait(S, "tabk")
+    wait(S, "Lt")
     for d in range(N):
-        act("gd", T.gd[:, d:96:8], T.tabk[:], 512.0 - 1024.0 * T0 * d, 1024.0)
-    wait(V, "C")
-    tr("TT", T.TT[:, 32:64], T.C[:, 11:395:12])
-    tr("TT", T.TT[:, 65:97], T.C[:, 23:407:12])
+        act("gd", T.gd[:, d:96:8], T.Lt[:, 16 * d:16 * d + 12], 512.0, -1024.0)
+    act("pb0", T.pb[:], T.e48[:, 0:64])
+    for h in range(2):
+        act("torc", T.win1[:, 208 * h:208 * h + 208], T.e48[:, 0:208], 0.0, 0.0)
+    wait(V, "C", "z0")
+    tr("TU", T.TT[:, 65:97], T.C[:, 31:543:16])
+    tr("TT", T.TT[:, 32:64], T.C[:, 15:527:16])
+    wait(V, "TU")
+    scan("bc", T.bc[:], T.TT[:, 65:129], T.TT[:, 97:161], -192.0, A.add, A.add)
     wait(V, "TT")
     scan("Sq", T.Sq[:], T.TT[:, 32:96], T.TT[:, 0:64], -4.5, A.add, A.subtract)
+    wait(V, "bc")
+    tr("bct", T.bct[:], T.bc[:, 32:64])
     wait(V, "Sq")
     tr("F", T.F[:], T.Sq[:, 32:64])
-    wait(S, "Sq")
-    act("bc", T.bc[:], T.Sq[:, 0:32], T.Sq[:, 31:32], 0.0)
+    mst = T.st[:, 8 * me:8 * me + 8]
+    wait(g, "bct")
+    ends, homes = T.bct[:, 0:8], halves(mine["home"])
+    fused([(out, "sst", ends, [(mine["hf"], T.relst[:])]), (homes[0], "sst", ends, [(mine["hc"], T.relst[:])]),
+           (homes[1], "sst", ends, [(mine["hs"], T.relst[:])])])
+    fused([(out, "sst", ends, [(ranks[2 * mine["direct"] + y], mst) for y in range(2)]),
+           (home, "sst", ends, [(ranks[mine["near"]], mst)])])
+    wait(V, "stage")
+    for e in range(2):
+        cp("offp", T.offp[:, e:4:2], T.stage[:, 9 + 12 * e:13 + 12 * e:2])
     wait(V, "F")
     wait(S, "F")
     for d in range(N):
-        if d == 1:
-            wait(V, "bc")
-            tr("bct", T.bct[:], T.bc[:])
-        if d < 5:
-            ts("td", T.td[:, d:96:8], T.C[:, 12 + 12 * d:24 + 12 * d], T.F[:, d:d + 1], None, A.add)
+        if d < 4:
+            ts("td", T.td[:, d:96:8], T.C[:, 16 + 16 * d:28 + 16 * d], T.F[:, d:d + 1], None, A.add)
         else:
-            act("td", T.td[:, d:96:8], T.C[:, 12 + 12 * d:24 + 12 * d], T.F[:, d:d + 1])
+            act("td", T.td[:, d:96:8], T.C[:, 16 + 16 * d:28 + 16 * d], T.F[:, d:d + 1])
+    quantize(0)
     wait(V, "td", "gd")
     scan("pos", T.pos[:], T.gd[:], T.td[:], 0.0, A.max, A.min)
-    mst = T.st[:, 8 * me:8 * me + 8]
-    wait(S, "bct")
-    act("sto", mst, T.bct[:, 0:8], 4.5 - 192.0)
     pos = T.pos[:, 7:96:8]
-    wait(S, "pos", "pb0")
+    wait(S, "bct")
+    for i, c in enumerate((0.0, 1.0, 1.0 - T0)):
+        act("e", T.e0[:, i:36:3], T.e48[:, 0:12], c, 0.0)
+    act("e", T.e1[:, 1:36:3], T.e48[:, 0:12], -float(ROUND), 0.0)
+    wait(S, "pos", "pb0", "k2")
+    act("par8", T.par8[:], T.epar[:], 8.0, -8.0)
     for b in range(3):
         act("pb", T.pb[32 * b:32 * b + 32, 0:64:16], T.pos[32 * b:32 * b + 32, 7 + 32 * b:32 + 32 * b:8], -188.5)
+    wait(S, "par8", "torc0")
+    act("torc", T.torc[:], T.torc[:], T.par8[:])
+    act("sto", mst, T.bct[:, 0:8])
+    act("kpb", T.kpb[:], T.kp[:], 512.0, 1024.0)
+    act("d1", T.da[:], T.epar[:], -2.0, 4.0)
+    act("d1", T.db[:], T.epar[:], 2.875, -1.0)
+    inc(S.activation(T.jw[:, 0:1], T.kp[:, 0:1], AF.Sign, -11.5), "f1")
+    inc(S.activation(T.jw[:, 1:2], T.kp[:, 0:1], AF.Relu, 7.0, -1.0), "f1")
+    act("cB", T.stf[:, 64:72], T.k16[:, 0:8], T0 / 8 + 0.4375 * N, 0.0)
+    act("cB", T.stf[:, 0:8], T.k16[:, 0:8], 0.0, 0.0)
+    act("f1", T.rst8[:], T.thr[:, 0:64], 1.0, 0.0)
+    act("f1", T.rstD[:], T.thr[:, 0:112], 0.0, 0.0)
+    act("X0", T.X[:], T.e48[:])
+    act("rst8", T.c8p[:, 0:1], T.thr[:, 0:1], 0.0, 0.0)
+    wait(S, "f1")
+    act("d1", T.jx[:, 0:1], T.kp[:, 0:1], T.jw[:, 0:1])
+    act("d1", T.jx[:, 1:2], T.jw[:, 1:2], 24.0, -1.0)
+    act("rst8", T.rst8[:, 0:64:8], T.thr[:, 0:8], 0.0, 0.0)
+    act("rstD", T.rstD[:, 0:112:8], T.thr[:, 0:14], -float(ROUND), 0.0)
+    wait(S, "cA0")
+    act("cB", T.cB[:], T.cA[:], 0.0, 0.0625)
+    quantize(1)
     wait(V, "pos")
     ts("qa", T.e1[:, 0:36:3], pos, 0.125, float(ROUND), A.mult, A.add)
     ts("qa", T.e1[:, 2:36:3], pos, 48.0, 184.0, A.mult, A.add)
     wait(V, "qa", "e")
     scan("e2", T.e2[:], T.e0[:], T.e1[:], 0.0, A.mult, A.add)
-    wait(V, "stage")
-    for e in range(2):
-        cp("prow", T.offp[:, e:4:2], T.stage[:, 9 + 12 * e:13 + 12 * e:2])
-    wait(V, "e2")
-    cp("off1", T.off1[:], T.e2[:, 2:36:3])
     wait(V, "pb")
     tr("prow", T.prow[:], T.pb[:])
-    wait(V, "prow", "win2")
+    wait(V, "e2")
+    cp("off1", T.off1[:], T.e2[:, 2:36:3])
+    wait(V, "prow", "offp", "win2")
     cp("places", T.win2[:].indirect(T.offp[:]), T.prow[:])
     wait(V, "off1", "torc")
     cp("win1", T.win1[:].indirect(T.off1[:]), T.torc[:])
-    wait(V, "x")
-    inc(V.quantize_mx(T.qx[:], T.sx[:], T.xt[:]), "qx")
+    quantize(2)
     wait(V, "win1")
     tr("trA", T.trA[:], T.win1[:])
     tr("trB", T.trB[:], T.win1[:, 16:400])
@@ -282,109 +317,92 @@ def rank_program(g, core, T, topo):
     wait(V, "g1", "qx")
     wait(S, "g1", "qx")
     own1 = slice(SW * me, SW * me + SW)
-    for i, h in enumerate((mine["split"] // 2, chip // 2)):
-        lst, cols = T.g1[:, 12 * h:12 * h + 13], slice(HALF * h, HALF * h + HALF)
+    for i, (a, k) in enumerate(((mine["split"], 7), (mine["carried"], 7), (chip & 2, 13))):
+        lst, cols = T.g1[:, 6 * a:6 * a + k], slice(PAIR * i, PAIR * i + 16 * k)
         cp("pk1c%d" % i, u32(T.slot1c[:, cols]), u32(T.qx[:]).indirect(lst))
         act("pk1s%d" % i, T.slot1s[:, cols], T.sx[:].indirect(lst))
-    cp("ownl", T.ownl[:], T.g1[:, 3 * me:3 * me + 4])
+        if i == 1:
+            cp("ownl", T.ownl[:], T.g1[:, 3 * me:3 * me + 4])
     wait(V, "ownl")
     cp("own1c", u32(T.land1c[:, own1]), u32(T.qx[:]).indirect(T.ownl[:]))
+    for q in (V, S):
+        q.wait_ge(T.sem.sst, n_st)
+        wait(q, "sto")
+    for d in range(1, N):
+        if d < 3:
+            ts("stf", T.stf[:, 8 * d:8 * d + 8], T.st[:, d - 1:64:8], 0.125, 24.0 + 0.4375 * d, A.mult, A.add)
+        else:
+            act("stf", T.stf[:, 8 * d:8 * d + 8], T.st[:, d - 1:64:8], 24.0 + 0.4375 * d, 0.125)
     wait(S, "ownl")
     act("own1s", T.land1s[:, own1], T.sx[:].indirect(T.ownl[:]))
 
     def send(ph, pair, single, land, rel, between=None):
-        for k in "cs":
-            wait(g, "pk%d%s0" % (ph, k))
-            fused([(out, "p%d%s" % (ph, k), pair(k, mine["split"]), [(mine["hf"], rel(k))]),
-                   (home, "p%d%s" % (ph, k), pair(k, mine["carried"]), [(mine["h" + k], rel(k))])])
         if between:
             between()
+        wait(g, "pk%dc0" % ph)
+        fused([(out, "p%dc" % ph, pair("c", mine["split"]), [(mine["hf"], rel("c"))])])
+        wait(g, "pk%dc1" % ph)
+        fused([(home, "p%dc" % ph, pair("c", mine["carried"]), [(mine["hc"], rel("c"))])])
+        wait(g, "pk%ds0" % ph, "pk%ds1" % ph)
+        fused([(out, "p%ds" % ph, pair("s", mine["split"]), [(mine["hf"], rel("s"))]),
+               (home, "p%ds" % ph, pair("s", mine["carried"]), [(mine["hs"], rel("s"))])])
         for k in "cs":
-            wait(g, "pk%d%s1" % (ph, k))
+            wait(g, "pk%d%s2" % (ph, k))
             fused([(outs[y], "p%d%s" % (ph, k), single(k, d), [(ranks[d], land(k, d))])
                    for y, d in enumerate((2 * mine["direct"], 2 * mine["direct"] + 1))]
                   + [(home, "p%d%s" % (ph, k), single(k, mine["near"]), [(ranks[mine["near"]], land(k, mine["near"]))])])
 
     def view(c, s):
         return lambda k, cols: u8(c[:, cols]) if k == "c" else s[:, cols]
-    wait(g, "sto")
-    fused([(out, "sst", mst, [(mine["hf"], T.relst[:])] + [(ranks[2 * mine["direct"] + y], mst) for y in range(2)]),
-           (home, "sst", mst, [(mine["hc"], T.relst[:]), (mine["hs"], T.relst[:]), (ranks[mine["near"]], mst)])])
-    iota("cA", T.cA[:], [[0, 8], [8 * SW, 8]], 7 - me)
-    iota("cA", T.stf[:, 64:72], [[0, 8]], T0)
-    iota("cA", T.rst8[:], [[0, 64]], 1)
-    iota("rst8", T.c8p[:, 0:1], [[0, 1]], 0)
-    wait(g, "cA")
-    iota("rst8", T.rst8[:, 0:64:8], [[0, 8]], 0)
-    iota("X0", T.X[:], [[0, 224]], EMPTY)
     wait(Y, "places")
     dma(Y, "pd", T.pd[:], T.win2[0:16 * NG:16, :])
+    dma(Y, "w", T.wt[:], T.w[:])
 
     def tables():
         wait(g, "pd")
-        far = [d for d in range(N) if d // 2 != chip]
-        ways = ([(mine["out"][i], d, ranks[d], T.lq[me]) for i, d in enumerate(far)]
-                + [(mine["home"][0], mine["near"], ranks[mine["near"]], T.lq[me]), (mine["home"][1], me, mine["hc"], T.rell[:])])
-        g.remote_dma_fused([RemoteDMATransfer(dst_ids=[dst_of(topo, c)], dma_engine_mask=1 << e, remote_sem=T.sem.sls, alu_op=2,
-                                              srcs=[T.pd[N * q + d] for q in range(NG)], dsts=[to]) for e, d, c, to in ways],
-                           local_sem=T.sem.loc)
+        g.remote_dma_fused([RemoteDMATransfer(dst_ids=[dst_of(topo, mine["hs"])], dma_engine_mask=1 << e, remote_sem=T.sem.sls,
+                                              alu_op=2, srcs=[T.pd[N * q + d] for q in range(NG)], dsts=[T.rell[d]])
+                            for d, e in enumerate(mine["home"])], local_sem=T.sem.loc)
         ln[0] += N
     v1, w1, r1 = view(T.slot1c, T.slot1s), view(T.land1c, T.land1s), view(T.rel1c, T.rel1s)
 
-    def at1(d):
-        return HALF * (d // 4) + Q1 * (d % 4)
-    send(1, lambda k, a: v1(k, slice(at1(2 * a), at1(2 * a) + Q1 + R1)), lambda k, d: v1(k, slice(at1(d), at1(d) + R1)),
-         lambda k, d: w1(k, slice(SW * me, SW * me + R1)), lambda k: r1(k, slice(0, Q1 + R1)), tables)
-    iota("rst0", T.rstD[:], [[0, 112]], 0)
-    wait(g, "rst0")
-    iota("rstD", T.rstD[:, 0:112:8], [[0, 14]], -ROUND)
+    def pair1(k, a):
+        b = PAIR * (a != mine["split"])
+        return v1(k, slice(b, b + Q1 + R1))
+    send(1, pair1, lambda k, d: v1(k, slice(2 * PAIR + Q1 * (d % 4), 2 * PAIR + Q1 * (d % 4) + R1)),
+         lambda k, d: w1(k, slice(SW * me, SW * me + R1)), lambda k: r1(k, slice(None)), tables)
     Y.wait_ge(T.sem.sls, N)
     wait(Y, "X0")
     for q in range(8):
         dma(Y, "X", T.X[16 * q:16 * q + 16, 16 * (q % 2):16 * (q % 2) + 192], T.lq[:])
 
-    for q in (V, S):
-        q.wait_ge(T.sem.sst, n_st)
-    wait(V, "sto")
-    for d in range(N):
-        if d < 5:
-            ts("stf", T.stf[:, 8 * d:8 * d + 8], T.st[:, d:64:8], 192.0, None, A.add)
-        else:
-            act("stf", T.stf[:, 8 * d:8 * d + 8], T.st[:, d:64:8], 192.0)
-    wait(V, "stf", "cA")
-    tt("l1", T.nn[:], T.stf[:, 0:64], T.stf[:, 8:72], A.subtract)
-    tt("l1", T.ai[:], T.stf[:, 0:64], T.cA[:], A.add)
-    wait(V, "l1")
-    ts("l2", T.ci[:], T.nn[:], 3, None, A.arith_shift_right)
-    ts("l3", T.ti[:], T.ai[:], 3, None, A.arith_shift_right)
+    wait(V, "stf", "cB")
+    tt("l2", T.ci[:], T.stf[:, 0:64], T.stf[:, 8:72], A.subtract)
     wait(V, "l2")
     cp("l3", T.c8p[:, 1:65], T.ci[:])
     wait(V, "l3", "rst8")
     scan("nB", T.nB[:], T.c8p[:, 0:64], T.rst8[:], 0.0, A.add, A.mult)
-    wait(V, "nB", "kpb")
-    wait(S, "nB")
+    tt("nB1", T.ti[:], T.stf[:, 0:64], T.cB[:], A.add)
+    wait(V, "nB", "nB1")
+    wait(S, "nB", "kpb")
     tt("ge0", T.tq[:], T.ti[:], T.nB[:], A.add)
     for kk in range(4):
-        ge = T.ge[:, 64 * kk:64 * kk + 64]
-        if kk < 2:
-            ts("ge0", ge, T.nB[:], 1024.0, T.kpb[:, kk:kk + 1], A.mult, A.add)
-        else:
-            act("ge2", ge, T.nB[:], T.kpb[:, kk:kk + 1], 1024.0)
+        act("ge%d" % kk, T.ge[:, 64 * kk:64 * kk + 64], T.nB[:], T.kpb[:, kk:kk + 1], 1024.0)
     for kk in range(4):
-        if kk % 2 == 0:
-            wait(V, "ge%d" % kk)
+        wait(V, "ge%d" % kk)
         scan("l7", T.sc[:, 64 * kk:64 * kk + 64], T.ge[:, 64 * kk:64 * kk + 64], T.tq[:], 0.0, A.max, A.min)
     wait(V, "l7")
     for kk in range(4):
         ts("off2", T.off2[:, kk:32:4], T.sc[:, 64 * kk + 7:64 * kk + 64:8], T.kp[:, kk:kk + 1], float(7 * SW + Q1), A.add, A.min)
+    tt("t8", T.t8[:], T.nB[:, 8 * me:8 * me + 8], T.stf[:, 8 * me:8 * me + 8], A.add)
 
     wait(V, "own1c", "off2")
-    V.wait_ge(T.sem.p1c, n_in)
+    V.wait_ge(T.sem.p1c, n_c)
     wait(S, "off2", "own1s")
-    S.wait_ge(T.sem.p1s, n_in)
+    S.wait_ge(T.sem.p1s, n_s)
     three = sorted((2 * mine["direct"], 2 * mine["direct"] + 1, mine["near"]))
-    runs = [(0, 4 * (mine["split"] // 2), 4)]
-    runs += [(1, three[0], 3)] if three[2] - three[0] == 2 else [(1, 2 * mine["direct"], 2), (1, mine["near"], 1)]
+    runs = [(0, 2 * mine["split"], 2), (1, 2 * mine["carried"], 2)]
+    runs += [(2, three[0], 3)] if three[2] - three[0] == 2 else [(2, 2 * mine["direct"], 2), (2, mine["near"], 1)]
     for i, d, k in runs:
         lst, cols = T.off2[:, 4 * d:4 * (d + k)], slice(SW * d, SW * (d + k))
         cp("pk2c%d" % i, u32(T.slot2c[:, cols]), u32(T.land1c[:]).indirect(lst))
@@ -393,28 +411,21 @@ def rank_program(g, core, T, topo):
     act("own2", T.land2s[:, 0:SW], T.land1s[:].indirect(T.off2[:, 4 * me:4 * me + 4]))
     v2, w2, r2 = view(T.slot2c, T.slot2s), view(T.land2c, T.land2s), view(T.rel2c, T.rel2s)
     send(2, lambda k, a: v2(k, slice(2 * SW * a, 2 * SW * a + SW + CAP)), lambda k, d: v2(k, slice(SW * d, SW * d + CAP)),
-         lambda k, d: w2(k, blk2(me, d)), lambda k: r2(k, slice(0, SW + CAP)))
+         lambda k, d: w2(k, blk2(me, d)), lambda k: r2(k, slice(None)))
 
-    ts("t8", T.t8[:], T.nB[:, 8 * me:8 * me + 8], -8.0, float(513 * 192 + 512 * (N - me)), A.mult, A.add)
-    wait(V, "w")
-    inc(V.quantize_mx(T.qw[:], T.sw[:], T.wt[:]), "qw")
+    ts("d1", T.pi1[:], T.pidx[:, 0:1], 1, None, A.bitwise_and)
     wait(V, "t8")
     for i in (0, 1, 16, 17):
-        tt("kin", T.kin[:, i:16 * (i // 16) + 16:2], T.t8[:], T.stf[:, 8 * me:8 * me + 8], A.subtract)
+        ts("kin", T.kin[:, i:16 * (i // 16) + 16:2], T.t8[:], -8.0, 513 * 192 + 512 * (N - me) + 3.5 * me, A.mult, A.add)
     wait(V, "kin")
     tr("kt", T.kt[:], T.kin[:])
-    ts("d1", T.pi1[:], T.pidx[:, 0:1], 1, None, A.bitwise_and)
-    ts("d1", T.da[:], T.epar[:], 4.0, -2.0, A.mult, A.add)
-    ts("d1", T.db[:], T.epar[:], -1.0, 1.875, A.mult, A.add)
-    ts("d1", T.j23[:], T.kp[:, 0:2], 23.0, None, A.min)
-    ts("d1", T.jw[:], T.kp[:, 0:2], 12.0, 2.0, A.is_ge, A.mult)
-    wait(V, "d1")
-    ts("d2", T.dl[:], T.pi1[:], T.da[:], T.db[:], A.mult, A.add)
-    tt("d2", T.jx[:], T.j23[:], T.jw[:], A.add)
-    wait(V, "d2")
-    ts("selD", T.selD[:], T.jx[:], T.dl[:], 8.0, A.add, A.mult)
     wait(S, "X", "kt")
     act("Xk", T.Xk[:], T.X[:], T.kt[:, 0:1], 513.0)
+    wait(V, "w", "d1")
+    ts("d2", T.dl[:], T.pi1[:], T.da[:], T.db[:], A.mult, A.add)
+    inc(V.quantize_mx(T.qw[:], T.sw[:], T.wt[:]), "qw")
+    wait(V, "d2")
+    ts("selD", T.selD[:], T.jx[:], T.dl[:], 8.0, A.add, A.mult)
     wait(V, "Xk")
     tr("Xt", T.Xt[:], T.Xk[:])
     wait(V, "Xt", "rstD")
@@ -427,19 +438,17 @@ def rank_program(g, core, T, topo):
     wait(V, "mk")
     cp("off5", T.off5[:], T.mi[:])
 
-    h2 = 8 + 4 * CAP
     wait(TE, "qw", "own2")
-    TE.wait_ge(T.sem.p2c, n_in)
-    TE.wait_ge(T.sem.p2s, n_in)
-    for h, (a, b) in enumerate(((0, h2), (h2, L2))):
-        inc(TE.matmul_mx(T.ps[:, 512 * h:512 * h + b - a], T.qw[:], T.sw[:], T.land2c[:, a:b], T.land2s[:, a:b], True, True),
-            "mm%d" % h)
-    wait(S, "mm0")
-    wait(V, "mm1")
-    for m in range(4):
-        a = 8 + CAP * m if m else 0
-        act("ysb", T.ysb[:, SW * m:SW * m + CAP], T.ps[:, a:a + CAP])
-        cp("ysb", T.ysb[:, SW * (m + 4):SW * (m + 4) + CAP], T.ps[:, 512 + CAP * m:512 + CAP * m + CAP])
+    TE.wait_ge(T.sem.p2c, n_c)
+    TE.wait_ge(T.sem.p2s, n_s)
+    for h in range(4):
+        a = min(2 * CAP * h + 8 * (h > 0), L2 - 128)
+        inc(TE.matmul_mx(T.ps[:, 512 * h:512 * h + 128], T.qw[:], T.sw[:], T.land2c[:, a:a + 128], T.land2s[:, a:a + 128],
+                         True, True), "mm%d" % h)
+        wait((S, V)[h % 2], "mm%d" % h)
+        for m in (2 * h, 2 * h + 1):
+            b = 512 * h + (8 + CAP * m if m else 0) - a
+            (act, cp)[h % 2]("ysb", T.ysb[:, SW * m:SW * m + CAP], T.ps[:, b:b + CAP])
     wait(V, "off5", "ysb")
     wait(S, "off5", "ysb")
     cp("yv", T.yo[:, 0:192], T.ysb[:].indirect(T.off5[:, 0:12]))

from concourse.bass import DstId, RemoteDMATransfer
from concourse.mybir import dt, AluOpType as A, ActivationFunctionType as AF

T0, N, Q1, CAP, SW = 384, 8, 48, 56, 64
R1 = Q1 + 1
PAIR, HALF = 2 * Q1 + 16, 4 * Q1 + 16
L2 = 8 + N * CAP
EMPTY = -1024
NG = 6
BIG = 65536.0
ROUND = 12582912
X4, U8, U16, F32, BF, I32 = "float8_e4m3fn_x4", "uint8", "uint16", "float32", "bfloat16", "int32"


def sb(n, t):
    return ("sbuf", [128, n], t)


SCRATCH = {
    "xt": sb(1536, BF), "wt": sb(512, BF), "qx": sb(T0, X4), "sx": sb(T0, U8), "qw": sb(128, X4), "sw": sb(128, U8),
    "slot1c": sb(2 * PAIR + HALF, X4), "slot1s": sb(2 * PAIR + HALF, U8), "land1c": sb(512, X4), "land1s": sb(512, U8),
    "slot2c": sb(N * SW, X4), "slot2s": sb(N * SW, U8), "land2c": sb(L2, X4), "land2s": sb(L2, U8),
    "relst": sb(8, BF), "rel1c": sb(Q1 + R1, X4), "rel1s": sb(Q1 + R1, U8), "rel2c": sb(SW + CAP, X4),
    "rel2s": sb(SW + CAP, U8),
    "tab": sb(16, I32), "Lt": sb(144, F32), "C": sb(544, F32), "thr": sb(128, F32), "l16": sb(8, U16),
    "TT": sb(161, F32), "Sq": sb(64, F32),
    "F": sb(32, F32), "bc": sb(64, BF), "bct": sb(32, BF), "gd": sb(96, F32), "td": sb(96, F32), "pos": sb(96, F32),
    "e0": sb(36, F32), "e1": sb(36, F32), "e2": sb(36, F32), "off1": sb(12, U16), "torc": sb(192, BF),
    "win1": sb(416, BF), "trA": sb(416, BF), "trB": sb(T0, BF), "U": sb(32, F32), "sel": sb(2, U16), "g1": sb(32, U16),
    "ownl": sb(4, U16), "pidx": sb(8, I32), "pi15": sb(8, I32), "pi16": sb(1, I32), "pi1": sb(1, I32),
    "par8": sb(1, F32), "epar": sb(1, F32), "k16": sb(8, F32), "kp": sb(4, F32), "kpb": sb(4, F32),
    "da": sb(1, F32), "db": sb(1, F32), "dl": sb(1, F32),
    "selD": sb(2, U16), "stage": sb(33, I32), "offp": sb(4, U16), "pb": sb(64, BF), "prow": sb(64, BF),
    "e48": sb(224, BF), "win2": sb(N * T0, BF), "X": sb(224, BF), "Xk": sb(224, F32), "Xt": sb(224, F32),
    "rstD": sb(112, F32), "Xs": sb(224, F32), "t8": sb(8, F32), "kin": sb(32, F32), "kt": sb(32, F32),
    "cd": sb(32, I32), "mi": sb(24, I32), "jw": sb(2, F32), "jx": sb(2, F32), "off5": sb(24, U16),
    "cA": sb(64, F32), "st": sb(64, BF), "stf": sb(72, F32), "cB": sb(64, F32),
    "ci": sb(64, I32), "ti": sb(64, I32), "c8p": sb(66, F32), "rst8": sb(64, F32), "nB": sb(64, F32),
    "ge": sb(256, F32), "tq": sb(64, F32), "sc": sb(256, F32), "off2": sb(32, U16), "ysb": sb(N * SW, F32), "yo": sb(T0, F32),
    "pd": ("dram", [N * NG, 128, 3], BF), "lq": ("dram", [N, 128, 3], BF), "rell": ("dram", [N, 128, 3], BF),
    "ps": ("psum", [128, 2048], F32),
}
SEMAPHORES = ["sst", "sls", "p1c", "p1s", "p2c", "p2s", "loc"] + ["s%d" % i for i in range(120)]


def bits(m):
    return bin(m).count("1")


def mask_of(es):
    return sum(1 << x for x in es)


def dst_of(topo, c):
    a = topo.addr(c)
    return DstId(rid=a[0], pnc=a[1])


def plan(topo, ranks, r):
    me, a = ranks[r], r // 2
    assert all(topo.chip(ranks[2 * i]) == topo.chip(ranks[2 * i + 1]) for i in range(N // 2))

    def hands(c):
        return [h for h in topo.cores_of(c) if h not in ranks and topo.die(h) == topo.die(c)]
    there = [ranks[q] for q in (2 * (a ^ 2), 2 * (a ^ 2) + 1) if topo.die(ranks[q]) == topo.die(me)][0]
    out = topo.engines(me, there)
    return {"direct": a ^ 1, "split": a ^ 2, "carried": a ^ 3, "near": r ^ 1, "hc": hands(me)[0], "hs": hands(me)[1],
            "hf": hands(there)[2], "out": out, "home": [x for x in topo.engines(me, ranks[r ^ 1]) if x not in out]}


def halves(es):
    return mask_of(es[:len(es) // 2]), mask_of(es[len(es) // 2:])


def u8(ap):
    return ap.bitcast(dt.uint8)


def u32(ap):
    return ap.bitcast(dt.uint32)


def blk2(s, d):
    b = 8 + CAP * ((s - d) % N)
    return slice(b, b + CAP)


def hand_on(g, core, T, topo, ranks, plans):
    for s in range(N):
        p = plans[s]
        if core not in (p["hc"], p["hs"], p["hf"]):
            continue
        a = p["split"] if core == p["hf"] else p["carried"]
        es = topo.engines(core, ranks[2 * a])
        ms = halves(es)
        l1, mst = slice(SW * s, SW * s + R1), T.st[:, 8 * s:8 * s + 8]
        two = (2 * a, 2 * a + 1)
        steps = {
            "p1c": [(d, ms[y], u8(T.rel1c[:, Q1 * y:Q1 * y + R1]), u8(T.land1c[:, l1])) for y, d in enumerate(two)],
            "p1s": [(d, ms[y], T.rel1s[:, Q1 * y:Q1 * y + R1], T.land1s[:, l1]) for y, d in enumerate(two)],
            "p2c": [(d, ms[y], u8(T.rel2c[:, SW * y:SW * y + CAP]), u8(T.land2c[:, blk2(s, d)])) for y, d in enumerate(two)],
            "p2s": [(d, ms[y], T.rel2s[:, SW * y:SW * y + CAP], T.land2s[:, blk2(s, d)]) for y, d in enumerate(two)]}
        m_in = len(p["home"])
        if core == p["hf"]:
            steps["sst"] = [(d, ms[y], T.relst[:], mst) for y, d in enumerate(two)]
            order = ["sst", "p1c", "p1s", "p2c", "p2s"]
        else:
            y = 0 if core == p["hc"] else 1
            steps["sst"] = [(two[y], ms[0] | ms[1], T.relst[:], mst)]
            steps["sls"] = [(d, 1 << es[d], T.rell[d], T.lq[s]) for d in range(N)]
            order = ["sst", "p1c", "p2c"] if y == 0 else ["sst", "sls", "p1s", "p2s"]
        for sem in order:
            g.wait_ge(T.sem[sem], m_in // 2 if sem == "sst" and core != p["hf"] else m_in)
            g.remote_dma_fused([RemoteDMATransfer(dst_ids=[dst_of(topo, ranks[d])], dma_engine_mask=m, remote_sem=T.sem[sem],
                                                  src=src, dst=dst) for d, m, src, dst in steps[sem]], local_sem=T.sem.loc)
        g.wait_ge(T.sem.loc, sum(bits(t[1]) for sem in order for t in steps[sem]))


def rank_program(g, core, T, topo):
    me = T.rank_of(core)
    ranks = list(T.cores)
    plans = [plan(topo, ranks, r) for r in range(N)]
    if me is None:
        hand_on(g, core, T, topo, ranks, plans)
        return
    V, S, Y, TE = g.vector, g.scalar, g.sync, g.tensor
    mine, par, chip = plans[me], me % 2, me // 2
    names, count, seen, ln = {}, {}, {}, [0]

    def inc(ins, name, n=1):
        names.setdefault(name, T.sem["s%d" % len(names)])
        ins.then_inc(names[name], n)
        count[name] = count.get(name, 0) + n

    def wait(q, *ns):
        for name in ns:
            q.wait_ge(names[name], count[name])
            seen[name] = count[name]

    def ts(name, out, in0, s1, s2, o0, o1=None):
        inc(V.tensor_scalar(out, in0, s1, s2, o0, o1) if o1 is not None else V.tensor_scalar(out, in0, s1, s2, o0), name)

    def tt(name, out, a, b, op):
        inc(V.tensor_tensor(out, a, b, op), name)

    def cp(name, out, in_):
        inc(V.tensor_copy(out, in_), name)

    def scan(name, out, a, b, init, o0, o1):
        inc(V.tensor_tensor_scan(out, a, b, init, o0, o1), name)

    def tr(name, out, in_):
        inc(V.transpose(out, in_), name)

    def fill(name, out, c):
        inc(V.memset(out, c), name)

    def act(name, out, in_, *bias_scale):
        inc(S.activation(out, in_, AF.Identity if bias_scale else AF.Copy, *bias_scale), name)

    def dma(q, name, out, in_):
        inc(q.dma_start(out, in_), name, 16)

    def iota(name, out, pat, b, cm=0):
        inc(g.iota(out, pat, b, cm, allow_small_or_imprecise_dtypes=True), name)

    def fused(trs):
        g.remote_dma_fused([RemoteDMATransfer(dst_ids=[dst_of(topo, c) for c, d in to], dma_engine_mask=m,
                                              remote_sem=T.sem[rs], srcs=[s], dsts=[d for c, d in to])
                            for m, rs, s, to in trs], local_sem=T.sem.loc)
        ln[0] += sum(bits(t[0]) for t in trs)

    out, home = mask_of(mine["out"]), mask_of(mine["home"])
    outs = halves(mine["out"])
    n_c = n_s = 2 * bits(outs[0]) + bits(home) + (bits(out) + bits(home)) + 2 * bits(outs[0])
    n_st = 2 * bits(out) + bits(home) + (bits(out) + bits(home)) + 2 * bits(out)

    for q in range(4):
        dma(Y if q % 2 == 0 else S, "tab", T.tab[32 * q:32 * q + 32, 0:12], T.to[:])

    def quantize(i):
        wait(V, "x%d" % i)
        inc(V.quantize_mx(T.qx[:, 128 * i:128 * i + 128], T.sx[:, 128 * i:128 * i + 128], T.xt[:, 512 * i:512 * i + 512]), "qx")
    iota("stage0", T.stage[:], [[1, 33]], 0, 24)
    iota("pidx", T.pidx[:], [[0, 8]], 0, 1)
    fill("e48", T.e48[:], float(EMPTY))
    wait(Y, "stage0")

    def stage(queue, e):
        for q in range(NG):
            u = 4 * (q // 2) + q % 2
            dma(queue, "stage", T.stage[16 * q:16 * q + 16, 9 - u + 12 * e:21 - u + 12 * e], T.to[8 * e:8 * e + 8, :])
    stage(Y, 0)
    wait(Y, "e48")
    dma(Y, "win2", T.win2[0:16 * NG:16, :], T.e48[0:16 * NG, 0:192])

    iota("thr", T.thr[:], [[T0, 8], [0, 16]], T0)
    iota("k16", T.k16[:], [[16, 8]], 0)
    iota("torc0", T.torc[:], [[16, 12], [1, 8], [192, 2]], -192)
    iota("cA0", T.cA[:], [[-7, 8], [16 * SW, 8]], 7 - 2 * me)
    fill("k0", T.tab[:, 12:16], N * T0)
    fill("k0", T.Lt[:, 0:16], 0.0)
    fill("k0", T.C[:, 15:544:16], 0.0)
    wait(V, "pidx")
    ts("k1", T.pi15[:], T.pidx[:], 15, None, A.bitwise_and)
    ts("k1", T.pi16[:], T.pidx[:, 0:1], 16, None, A.bitwise_and)
    wait(V, "k1")
    cp("k0", T.l16[:], T.pi15[:])
    ts("k2", T.epar[:], T.pi16[:], -0.0625, 1.0, A.mult, A.add)
    dma(S, "x0", T.xt[:, 0:512], T.x[:, 0:512])
    wait(S, "stage0")
    stage(S, 1)
    for i in (1, 2):
        dma(S, "x%d" % i, T.xt[:, 512 * i:512 * i + 512], T.x[:, 512 * i:512 * i + 512])
    wait(S, "e48")
    act("z0", T.TT[:], T.e48[:, 0:161], 0.0, 0.0)

    wait(V, "tab", "k0", "thr")
    tt("Lt", T.Lt[:, 16:144], T.tab[:].indirect(T.l16[:]), T.thr[:], A.is_lt)
    wait(V, "k16")
    tt("k2", T.kp[:], T.pi15[:, 0:4], T.k16[:, 0:4], A.add)
    wait(V, "Lt")
    scan("C", T.C[:, 16:144], T.Lt[:, 16:144], T.Lt[:, 0:128], 0.0, A.add, A.subtract)
    wait(V, "k2")
    ts("sel", T.sel[:], T.kp[:, 0:2], 23.0, T.epar[:], A.min, A.add)
    wait(S, "Lt")
    for d in range(N):
        act("gd", T.gd[:, d:96:8], T.Lt[:, 16 * d:16 * d + 12], 512.0, -1024.0)
    act("pb0", T.pb[:], T.e48[:, 0:64])
    for h in range(2):
        act("torc", T.win1[:, 208 * h:208 * h + 208], T.e48[:, 0:208], 0.0, 0.0)
    wait(V, "C", "z0")
    tr("TU", T.TT[:, 65:97], T.C[:, 31:543:16])
    tr("TT", T.TT[:, 32:64], T.C[:, 15:527:16])
    wait(V, "TU")
    scan("bc", T.bc[:], T.TT[:, 65:129], T.TT[:, 97:161], -192.0, A.add, A.add)
    wait(V, "TT")
    scan("Sq", T.Sq[:], T.TT[:, 32:96], T.TT[:, 0:64], -4.5, A.add, A.subtract)
    wait(V, "bc")
    tr("bct", T.bct[:], T.bc[:, 32:64])
    wait(V, "Sq")
    tr("F", T.F[:], T.Sq[:, 32:64])
    mst = T.st[:, 8 * me:8 * me + 8]
    wait(g, "bct")
    ends, homes = T.bct[:, 0:8], halves(mine["home"])
    fused([(out, "sst", ends, [(mine["hf"], T.relst[:])]), (homes[0], "sst", ends, [(mine["hc"], T.relst[:])]),
           (homes[1], "sst", ends, [(mine["hs"], T.relst[:])])])
    fused([(out, "sst", ends, [(ranks[2 * mine["direct"] + y], mst) for y in range(2)]),
           (home, "sst", ends, [(ranks[mine["near"]], mst)])])
    wait(V, "stage")
    for e in range(2):
        cp("offp", T.offp[:, e:4:2], T.stage[:, 9 + 12 * e:13 + 12 * e:2])
    wait(V, "F")
    wait(S, "F")
    for d in range(N):
        if d < 4:
            ts("td", T.td[:, d:96:8], T.C[:, 16 + 16 * d:28 + 16 * d], T.F[:, d:d + 1], None, A.add)
        else:
            act("td", T.td[:, d:96:8], T.C[:, 16 + 16 * d:28 + 16 * d], T.F[:, d:d + 1])
    quantize(0)
    wait(V, "td", "gd")
    scan("pos", T.pos[:], T.gd[:], T.td[:], 0.0, A.max, A.min)
    pos = T.pos[:, 7:96:8]
    wait(S, "bct")
    for i, c in enumerate((0.0, 1.0, 1.0 - T0)):
        act("e", T.e0[:, i:36:3], T.e48[:, 0:12], c, 0.0)
    act("e", T.e1[:, 1:36:3], T.e48[:, 0:12], -float(ROUND), 0.0)
    wait(S, "pos", "pb0", "k2")
    act("par8", T.par8[:], T.epar[:], 8.0, -8.0)
    for b in range(3):
        act("pb", T.pb[32 * b:32 * b + 32, 0:64:16], T.pos[32 * b:32 * b + 32, 7 + 32 * b:32 + 32 * b:8], -188.5)
    wait(S, "par8", "torc0")
    act("torc", T.torc[:], T.torc[:], T.par8[:])
    act("sto", mst, T.bct[:, 0:8])
    act("kpb", T.kpb[:], T.kp[:], 512.0, 1024.0)
    act("d1", T.da[:], T.epar[:], -2.0, 4.0)
    act("d1", T.db[:], T.epar[:], 2.875, -1.0)
    inc(S.activation(T.jw[:, 0:1], T.kp[:, 0:1], AF.Sign, -11.5), "f1")
    inc(S.activation(T.jw[:, 1:2], T.kp[:, 0:1], AF.Relu, 7.0, -1.0), "f1")
    act("cB", T.stf[:, 64:72], T.k16[:, 0:8], T0 / 8 + 0.4375 * N, 0.0)
    act("cB", T.stf[:, 0:8], T.k16[:, 0:8], 0.0, 0.0)
    act("f1", T.rst8[:], T.thr[:, 0:64], 1.0, 0.0)
    act("f1", T.rstD[:], T.thr[:, 0:112], 0.0, 0.0)
    act("X0", T.X[:], T.e48[:])
    act("rst8", T.c8p[:, 0:1], T.thr[:, 0:1], 0.0, 0.0)
    wait(S, "f1")
    act("d1", T.jx[:, 0:1], T.kp[:, 0:1], T.jw[:, 0:1])
    act("d1", T.jx[:, 1:2], T.jw[:, 1:2], 24.0, -1.0)
    act("rst8", T.rst8[:, 0:64:8], T.thr[:, 0:8], 0.0, 0.0)
    act("rstD", T.rstD[:, 0:112:8], T.thr[:, 0:14], -float(ROUND), 0.0)
    wait(S, "cA0")
    act("cB", T.cB[:], T.cA[:], 0.0, 0.0625)
    quantize(1)
    wait(V, "pos")
    ts("qa", T.e1[:, 0:36:3], pos, 0.125, float(ROUND), A.mult, A.add)
    ts("qa", T.e1[:, 2:36:3], pos, 48.0, 184.0, A.mult, A.add)
    wait(V, "qa", "e")
    scan("e2", T.e2[:], T.e0[:], T.e1[:], 0.0, A.mult, A.add)
    wait(V, "pb")
    tr("prow", T.prow[:], T.pb[:])
    wait(V, "e2")
    cp("off1", T.off1[:], T.e2[:, 2:36:3])
    wait(V, "prow", "offp", "win2")
    cp("places", T.win2[:].indirect(T.offp[:]), T.prow[:])
    wait(V, "off1", "torc")
    cp("win1", T.win1[:].indirect(T.off1[:]), T.torc[:])
    quantize(2)
    wait(V, "win1")
    tr("trA", T.trA[:], T.win1[:])
    tr("trB", T.trB[:], T.win1[:, 16:400])
    wait(V, "trA")
    tt("U", T.U[:, 0:25:2], T.trA[:, 0:416:32], T.trA[:, 16:416:32], A.add)
    wait(V, "trB")
    tt("U", T.U[:, 1:25:2], T.trB[:, 0:T0:32], T.trB[:, 16:T0:32], A.add)
    wait(V, "U", "sel")
    ts("g1", T.g1[:], T.U[:, 0:25].indirect(T.sel[:]), 192.0, None, A.add)
    wait(V, "g1", "qx")
    wait(S, "g1", "qx")
    own1 = slice(SW * me, SW * me + SW)
    for i, (a, k) in enumerate(((mine["split"], 7), (mine["carried"], 7), (chip & 2, 13))):
        lst, cols = T.g1[:, 6 * a:6 * a + k], slice(PAIR * i, PAIR * i + 16 * k)
        cp("pk1c%d" % i, u32(T.slot1c[:, cols]), u32(T.qx[:]).indirect(lst))
        act("pk1s%d" % i, T.slot1s[:, cols], T.sx[:].indirect(lst))
        if i == 1:
            cp("ownl", T.ownl[:], T.g1[:, 3 * me:3 * me + 4])
    wait(V, "ownl")
    cp("own1c", u32(T.land1c[:, own1]), u32(T.qx[:]).indirect(T.ownl[:]))
    for q in (V, S):
        q.wait_ge(T.sem.sst, n_st)
        wait(q, "sto")
    for d in range(1, N):
        if d < 3:
            ts("stf", T.stf[:, 8 * d:8 * d + 8], T.st[:, d - 1:64:8], 0.125, 24.0 + 0.4375 * d, A.mult, A.add)
        else:
            act("stf", T.stf[:, 8 * d:8 * d + 8], T.st[:, d - 1:64:8], 24.0 + 0.4375 * d, 0.125)
    wait(S, "ownl")
    act("own1s", T.land1s[:, own1], T.sx[:].indirect(T.ownl[:]))

    def send(ph, pair, single, land, rel, between=None):
        if between:
            between()
        wait(g, "pk%dc0" % ph)
        fused([(out, "p%dc" % ph, pair("c", mine["split"]), [(mine["hf"], rel("c"))])])
        wait(g, "pk%dc1" % ph)
        fused([(home, "p%dc" % ph, pair("c", mine["carried"]), [(mine["hc"], rel("c"))])])
        wait(g, "pk%ds0" % ph, "pk%ds1" % ph)
        fused([(out, "p%ds" % ph, pair("s", mine["split"]), [(mine["hf"], rel("s"))]),
               (home, "p%ds" % ph, pair("s", mine["carried"]), [(mine["hs"], rel("s"))])])
        for k in "cs":
            wait(g, "pk%d%s2" % (ph, k))
            fused([(outs[y], "p%d%s" % (ph, k), single(k, d), [(ranks[d], land(k, d))])
                   for y, d in enumerate((2 * mine["direct"], 2 * mine["direct"] + 1))]
                  + [(home, "p%d%s" % (ph, k), single(k, mine["near"]), [(ranks[mine["near"]], land(k, mine["near"]))])])

    def view(c, s):
        return lambda k, cols: u8(c[:, cols]) if k == "c" else s[:, cols]
    wait(Y, "places")
    dma(Y, "pd", T.pd[:], T.win2[0:16 * NG:16, :])
    dma(Y, "w", T.wt[:], T.w[:])

    def tables():
        wait(g, "pd")
        g.remote_dma_fused([RemoteDMATransfer(dst_ids=[dst_of(topo, mine["hs"])], dma_engine_mask=1 << e, remote_sem=T.sem.sls,
                                              alu_op=2, srcs=[T.pd[N * q + d] for q in range(NG)], dsts=[T.rell[d]])
                            for d, e in enumerate(mine["home"])], local_sem=T.sem.loc)
        ln[0] += N
    v1, w1, r1 = view(T.slot1c, T.slot1s), view(T.land1c, T.land1s), view(T.rel1c, T.rel1s)

    def pair1(k, a):
        b = PAIR * (a != mine["split"])
        return v1(k, slice(b, b + Q1 + R1))
    send(1, pair1, lambda k, d: v1(k, slice(2 * PAIR + Q1 * (d % 4), 2 * PAIR + Q1 * (d % 4) + R1)),
         lambda k, d: w1(k, slice(SW * me, SW * me + R1)), lambda k: r1(k, slice(None)), tables)
    Y.wait_ge(T.sem.sls, N)
    wait(Y, "X0")
    for q in range(8):
        dma(Y, "X", T.X[16 * q:16 * q + 16, 16 * (q % 2):16 * (q % 2) + 192], T.lq[:])

    wait(V, "stf", "cB")
    tt("l2", T.ci[:], T.stf[:, 0:64], T.stf[:, 8:72], A.subtract)
    wait(V, "l2")
    cp("l3", T.c8p[:, 1:65], T.ci[:])
    wait(V, "l3", "rst8")
    scan("nB", T.nB[:], T.c8p[:, 0:64], T.rst8[:], 0.0, A.add, A.mult)
    tt("nB1", T.ti[:], T.stf[:, 0:64], T.cB[:], A.add)
    wait(V, "nB", "nB1")
    wait(S, "nB", "kpb")
    tt("ge0", T.tq[:], T.ti[:], T.nB[:], A.add)
    for kk in range(4):
        act("ge%d" % kk, T.ge[:, 64 * kk:64 * kk + 64], T.nB[:], T.kpb[:, kk:kk + 1], 1024.0)
    for kk in range(4):
        wait(V, "ge%d" % kk)
        scan("l7", T.sc[:, 64 * kk:64 * kk + 64], T.ge[:, 64 * kk:64 * kk + 64], T.tq[:], 0.0, A.max, A.min)
    wait(V, "l7")
    for kk in range(4):
        ts("off2", T.off2[:, kk:32:4], T.sc[:, 64 * kk + 7:64 * kk + 64:8], T.kp[:, kk:kk + 1], float(7 * SW + Q1), A.add, A.min)
    tt("t8", T.t8[:], T.nB[:, 8 * me:8 * me + 8], T.stf[:, 8 * me:8 * me + 8], A.add)

    wait(V, "own1c", "off2")
    V.wait_ge(T.sem.p1c, n_c)
    wait(S, "off2", "own1s")
    S.wait_ge(T.sem.p1s, n_s)
    three = sorted((2 * mine["direct"], 2 * mine["direct"] + 1, mine["near"]))
    runs = [(0, 2 * mine["split"], 2), (1, 2 * mine["carried"], 2)]
    runs += [(2, three[0], 3)] if three[2] - three[0] == 2 else [(2, 2 * mine["direct"], 2), (2, mine["near"], 1)]
    for i, d, k in runs:
        lst, cols = T.off2[:, 4 * d:4 * (d + k)], slice(SW * d, SW * (d + k))
        cp("pk2c%d" % i, u32(T.slot2c[:, cols]), u32(T.land1c[:]).indirect(lst))
        act("pk2s%d" % i, T.slot2s[:, cols], T.land1s[:].indirect(lst))
    cp("own2", u32(T.land2c[:, 0:SW]), u32(T.land1c[:]).indirect(T.off2[:, 4 * me:4 * me + 4]))
    act("own2", T.land2s[:, 0:SW], T.land1s[:].indirect(T.off2[:, 4 * me:4 * me + 4]))
    v2, w2, r2 = view(T.slot2c, T.slot2s), view(T.land2c, T.land2s), view(T.rel2c, T.rel2s)
    send(2, lambda k, a: v2(k, slice(2 * SW * a, 2 * SW * a + SW + CAP)), lambda k, d: v2(k, slice(SW * d, SW * d + CAP)),
         lambda k, d: w2(k, blk2(me, d)), lambda k: r2(k, slice(None)))

    ts("d1", T.pi1[:], T.pidx[:, 0:1], 1, None, A.bitwise_and)
    wait(V, "t8")
    for i in (0, 1, 16, 17):
        ts("kin", T.kin[:, i:16 * (i // 16) + 16:2], T.t8[:], -8.0, 513 * 192 + 512 * (N - me) + 3.5 * me, A.mult, A.add)
    wait(V, "kin")
    tr("kt", T.kt[:], T.kin[:])
    wait(S, "X", "kt")
    act("Xk", T.Xk[:], T.X[:], T.kt[:, 0:1], 513.0)
    wait(V, "w", "d1")
    ts("d2", T.dl[:], T.pi1[:], T.da[:], T.db[:], A.mult, A.add)
    inc(V.quantize_mx(T.qw[:], T.sw[:], T.wt[:]), "qw")
    wait(V, "d2")
    ts("selD", T.selD[:], T.jx[:], T.dl[:], 8.0, A.add, A.mult)
    wait(V, "Xk")
    tr("Xt", T.Xt[:], T.Xk[:])
    wait(V, "Xt", "rstD")
    for w in range(2):
        scan("Xs", T.Xs[:, 112 * w:112 * w + 112], T.rstD[:], T.Xt[:, w:224:2], 0.0, A.add, A.max)
    wait(V, "Xs", "selD")
    cp("cd", T.cd[:], T.Xs[:].indirect(T.selD[:]))
    wait(V, "cd")
    ts("mk", T.mi[:], T.cd[:, 0:24], 3, N * SW - 1, A.logical_shift_right, A.bitwise_and)
    wait(V, "mk")
    cp("off5", T.off5[:], T.mi[:])

    wait(TE, "qw", "own2")
    TE.wait_ge(T.sem.p2c, n_c)
    TE.wait_ge(T.sem.p2s, n_s)
    for h in range(4):
        a = min(2 * CAP * h + 8 * (h > 0), L2 - 128)
        inc(TE.matmul_mx(T.ps[:, 512 * h:512 * h + 128], T.qw[:], T.sw[:], T.land2c[:, a:a + 128], T.land2s[:, a:a + 128],
                         True, True), "mm%d" % h)
        wait((S, V)[h % 2], "mm%d" % h)
        for m in (2 * h, 2 * h + 1):
            b = 512 * h + (8 + CAP * m if m else 0) - a
            (act, cp)[h % 2]("ysb", T.ysb[:, SW * m:SW * m + CAP], T.ps[:, b:b + CAP])
    wait(V, "off5", "ysb")
    wait(S, "off5", "ysb")
    cp("yv", T.yo[:, 0:192], T.ysb[:].indirect(T.off5[:, 0:12]))
    act("ys", T.yo[:, 192:T0], T.ysb[:].indirect(T.off5[:, 12:24]))
    wait(Y, "yv")
    dma(Y, "y", T.y[:, 0:192], T.yo[:, 0:192])
    wait(S, "ys")
    dma(S, "y", T.y[:, 192:T0], T.yo[:, 192:T0])
    wait(Y, "y")
    assert seen == count
    g.wait_ge(T.sem.loc, ln[0])
